import numpy as np
import ml_dtypes


def mxq(x, axis, fmt="e4m3"):
    dtype, down = {"e4m3": (ml_dtypes.float8_e4m3fn, 7), "e5m2": (ml_dtypes.float8_e5m2, 14)}[fmt]
    v = np.moveaxis(np.asarray(x, np.float32).astype(ml_dtypes.bfloat16).astype(np.float64), axis, -1)
    blocks = v.reshape(v.shape[:-1] + (-1, 32))
    amax = np.abs(blocks).max(-1, keepdims=True)
    byte = np.maximum(np.where(amax > 0, np.frexp(amax)[1] - 1 + 127, 0) - down, 1)
    scale = np.exp2(byte - 127.0)
    codes = (blocks / scale).astype(np.float32).astype(dtype).astype(np.float64)
    return np.moveaxis((codes * scale).reshape(v.shape), -1, axis)


WIDE = False


def mx_kscale(k):
    if not WIDE:
        return np.ones(k)
    levels = np.array([10, -10, 5, -5, 0])
    if k % 512:
        return np.exp2(np.random.permutation(np.resize(levels, k // 32))).repeat(32)
    a = np.empty((k // 512, 16))
    for p in range(k // 512):
        a[p, :8] = np.random.permutation(np.resize(levels, 8))
        for g in range(8):
            far = levels[np.abs(levels - a[p, g]) >= 10]
            a[p, g + 8] = far[np.random.randint(len(far))]
    return np.exp2(a.ravel()).repeat(32)


def f64(x):
    return np.asarray(x).astype(np.float64)


def striped(idx):
    return np.tile(idx.reshape(-1, 16).T, (8, 1)).astype(np.uint16)


def unstriped(offs):
    return offs[:16].T.reshape(-1).astype(np.int64)


E2M1 = np.array([0.0, 0.5, 1.0, 1.5, 2.0, 3.0, 4.0, 6.0, -0.0, -0.5, -1.0, -1.5, -2.0, -3.0, -4.0, -6.0])


def pack_weight(w, fmt):
    k, n = w.shape
    w = f64(np.asarray(w, np.float32).astype(ml_dtypes.bfloat16)).reshape(k // 32, 32, n)
    amax = np.abs(w).max(1)
    if fmt == "e4m3":
        byte = np.frexp(amax)[1] - 1 + 127 - 7
    else:
        mant, ex = np.frexp(amax / 6.0)
        byte = np.where(mant > 0.5, ex, ex - 1) + 127
    byte = np.clip(np.where(amax > 0, byte, 1), 1, 254)
    scaled = (w * np.exp2(127.0 - byte)[:, None, :]).reshape(k, n).astype(np.float32)
    by_word = np.ascontiguousarray(scaled.reshape(k // 512, 128, 4, n).transpose(0, 1, 3, 2))
    if fmt == "e4m3":
        words = by_word.astype(ml_dtypes.float8_e4m3fn).view(np.uint8)
    else:
        c = by_word.astype(ml_dtypes.float4_e2m1fn).view(np.uint8) & 0xF
        words = (c[..., 0::2] | (c[..., 1::2] << 4)).reshape(k // 512, 128, 2 * n)
    return np.ascontiguousarray(words), np.ascontiguousarray(byte.astype(np.uint8).reshape(k // 512, 16, n))


def unpack_weight(words, scales, fmt):
    g, _, n = scales.shape
    words = np.ascontiguousarray(words).reshape(g, 128, n, -1)
    if fmt == "e4m3":
        vals = words.view(ml_dtypes.float8_e4m3fn).astype(np.float64)
    else:
        nib = np.empty((g, 128, n, 4), np.uint8)
        nib[..., 0::2] = words & 0xF
        nib[..., 1::2] = words >> 4
        vals = E2M1[nib]
    vals = vals * np.repeat(np.exp2(scales.astype(np.float64) - 127.0), 8, axis=1)[..., None]
    return vals.transpose(0, 1, 3, 2).reshape(g * 512, n)


def gelu(v):
    return 0.5 * v * (1.0 + np.tanh(np.sqrt(2.0 / np.pi) * (v + 0.044715 * v**3)))


K, H, T, S, T2, T3, S2, P = 512, 1024, 4096, 1024, 2048, 2048, 512, 1024

def setup_inputs():
    n = np.random.standard_normal
    s = mx_kscale(K)[:, None]
    u = mx_kscale(H)[:, None]
    tab_words, tab_scales = pack_weight(n((K, T)) * s, "e4m3")
    tab2_words, tab2_scales = pack_weight(n((H, T3)) / np.sqrt(H) / u, "e4m3")
    w4_words, w4_scales = pack_weight(0.4 * n((K, H)) / np.sqrt(K) / s, "e2m1")
    return {
        "tab_words": tab_words, "tab_scales": tab_scales,
        "offs": striped(np.random.permutation(T)[:S]),
        "tab2_words": tab2_words, "tab2_scales": tab2_scales,
        "offs2": striped(np.random.permutation(T3)[:S2]),
        "w4_words": w4_words, "w4_scales": w4_scales,
        "w1": (0.3 * n((K, H)) / np.sqrt(K) / s).astype(np.float32),
        "gain": (np.exp(0.3 * n(H)) * u[:, 0]).astype(np.float32),
        "page0": (n((H, T2)) * u).astype(np.float32),
        "wgs": np.exp(0.3 * n((128, S))).astype(np.float32),
        "offs3": striped(np.random.permutation(T2)[:S]),
        "offs4": striped(np.random.permutation(T2)[:P]),
        "low": (0.5 * n(S2)).astype(np.float32),
    }

def reference(tab_words, tab_scales, offs, tab2_words, tab2_scales, offs2, w4_words, w4_scales,
              w1, gain, page0, wgs, offs3, offs4, low):
    v = unpack_weight(tab_words, tab_scales, "e4m3")[:, unstriped(offs)]
    v2 = unpack_weight(tab2_words, tab2_scales, "e4m3")[:, unstriped(offs2)]
    w4 = unpack_weight(w4_words, w4_scales, "e2m1")
    a = w4.T @ v + mxq(f64(w1), 0, "e4m3").T @ v
    h = f64(gain)[:, None] * (np.sin(a) + np.cos(a))
    page = f64(page0).copy()
    page[:, unstriped(offs3)] = np.tile(f64(wgs), (H // 128, 1)) * h
    e = v2.T @ mxq(page, 0, "e4m3")
    x = e[:, unstriped(offs4)]
    return np.square(np.maximum(x, f64(low)[:, None]))

@@ -1,0 +1,297 @@
+import math
+from contextlib import ExitStack
+
+import concourse.mybir as mybir
+from concourse.masks import make_identity
+
+K, H, T, S, T2, T3, S2, PICKS = 512, 1024, 4096, 1024, 2048, 2048, 512, 1024
+FLOPS = 2 * (2 * K * H * S + H * S2 * T2)
+
+F32 = mybir.dt.float32
+BF16 = mybir.dt.bfloat16
+I32 = mybir.dt.int32
+U32 = mybir.dt.uint32
+U16 = mybir.dt.uint16
+U8 = mybir.dt.uint8
+FP8X4 = mybir.dt.float8_e4m3fn_x4
+FP4X4 = mybir.dt.float4_e2m1fn_x4
+ACT = mybir.ActivationFunctionType
+ALU = mybir.AluOpType
+
+P = 128
+PACK = 4
+BANK = 512
+STRIPE = 16
+ROW_TILES = H // P
+PASSES = H // (P * PACK)
+CHUNKS = T2 // BANK
+CALL_TILES = S2 // P
+LAST = ROW_TILES - 1
+W1_LOADS = ((0, 256), (256, 1024))
+W1_GROUPS = ((0, 128), (128, 256), (256, 512), (512, 1024))
+AHEAD = 2
+
+
+def tile_list_birdsong_retrieval_kernel(
+    tc, tab_words, tab_scales, offs, tab2_words, tab2_scales, offs2, w4_words, w4_scales,
+    w1, gain, page0, wgs, offs3, offs4, low, out,
+):
+    nc = tc.nc
+    with ExitStack() as ctx:
+        lists = ctx.enter_context(tc.tile_pool(name="lists", bufs=1))
+        keep = ctx.enter_context(tc.tile_pool(name="keep", bufs=1))
+        ring = ctx.enter_context(tc.tile_pool(name="ring", bufs=1))
+        psum = ctx.enter_context(tc.psum_pool(name="psum", bufs=1))
+
+        def load_list(name, source):
+            tile = lists.tile(list(source.shape), U16, name=name)
+            nc.sync.dma_start(tile[:], source)
+            return tile
+
+        def part_of(list_tile, first, count):
+            return list_tile[:, first // STRIPE : (first + count) // STRIPE]
+
+        def load_scale_rows(engine, plane, source):
+            rows = 4 * source.shape[0]
+            for quad in range(4):
+                engine.dma_start(
+                    out=plane[32 * quad : 32 * quad + rows, :].bitcast(I32),
+                    in_=source[:, 4 * quad : 4 * quad + 4, :].bitcast(I32),
+                )
+
+        tab_plane = keep.tile([P, T], U8, name="tab_plane", align_bytes=64)
+        nc.vector.memset(tab_plane[:].bitcast(I32), 0)
+        w4_plane = keep.tile([P, H], U8, name="w4_plane", align_bytes=64)
+        nc.vector.memset(w4_plane[:].bitcast(I32), 0)
+        zero = keep.tile([P, 1], F32, name="zero")
+        nc.vector.memset(zero[:], 0.0)
+        half_amp = keep.tile([P, 1], F32, name="half_amp")
+        nc.scalar.activation(out=half_amp[:], in_=zero[:], func=ACT.Sin, bias=math.pi / 4)
+        tab2_plane = keep.tile([P, T3], U8, name="tab2_plane", align_bytes=64)
+        nc.vector.memset(tab2_plane[:].bitcast(I32), 0)
+
+        vectors = keep.tile([P, P], F32, name="vectors")
+        nc.gpsimd.memset(vectors[:], 0.0)
+        ident = keep.tile([P, P], F32, name="ident")
+        make_identity(nc, ident[:])
+        nc.gpsimd.dma_start(out=vectors[0:ROW_TILES, :], in_=gain.rearrange("(b p) -> b p", p=P))
+        nc.gpsimd.dma_start(out=vectors[ROW_TILES : ROW_TILES + CALL_TILES, :], in_=low.rearrange("(n p) -> n p", p=P))
+
+        w1_raw = []
+
+        def load_w1(i):
+            lo, hi = W1_LOADS[i]
+            raw = keep.tile([P, PACK, hi - lo], F32, name="w1_raw%d" % i)
+            nc.sync.dma_start(out=raw[:], in_=w1[:, lo:hi].rearrange("(p j) c -> p j c", j=PACK))
+            w1_raw.append(raw)
+
+        pages = []
+
+        def load_page(b):
+            page = ring.tile([P, T2], F32, name="page", tag="rows", bufs=4)
+            nc.sync.dma_start(out=page[:], in_=page0[P * b : P * (b + 1), :])
+            pages.append(page)
+
+        clip_list = load_list("clip_list", offs)
+        w4_tile = keep.tile([P, 2 * H], U8, name="w4_tile", align_bytes=64)
+        nc.sync.dma_start(out=w4_tile[:].bitcast(I32), in_=w4_words[0].bitcast(I32))
+        load_w1(0)
+        load_scale_rows(nc.sync, tab_plane, tab_scales)
+        tab_tile = keep.tile([P, T], U32, name="tab_tile", align_bytes=64)
+        nc.sync.dma_start(out=tab_tile[:].bitcast(I32), in_=tab_words[0].rearrange("p t i -> p (t i)").bitcast(I32))
+        load_scale_rows(nc.sync, w4_plane, w4_scales)
+        wgs_tile = ring.tile([P, S], F32, name="wgs_tile", tag="wgs", align_bytes=64)
+        nc.sync.dma_start(out=wgs_tile[:], in_=wgs)
+        place_list = load_list("place_list", offs3)
+        load_page(0)
+        load_w1(1)
+        load_page(1)
+        load_page(2)
+        load_page(3)
+        tab2_tiles = []
+        for a in range(PASSES):
+            words = keep.tile([P, T3], U32, name="tab2_tile%d" % a, align_bytes=64)
+            nc.sync.dma_start(out=words[:].bitcast(I32), in_=tab2_words[a].rearrange("p t i -> p (t i)").bitcast(I32))
+            tab2_tiles.append(words)
+        load_scale_rows(nc.sync, tab2_plane, tab2_scales)
+        call_list = load_list("call_list", offs2)
+        read_list = load_list("read_list", offs4)
+
+        banks = [psum.tile([P, BANK], F32, name="bank%d" % i) for i in range(8)]
+        columns = banks[7]
+        nc.tensor.transpose(columns[:, 0:P], vectors[:], ident[:])
+        amp_gain = keep.tile([P, ROW_TILES], F32, name="amp_gain")
+        nc.vector.tensor_scalar(amp_gain[:], columns[:, 0:ROW_TILES], half_amp[:], 2.0, ALU.mult, ALU.mult)
+        floor = keep.tile([P, CALL_TILES], F32, name="floor")
+        nc.vector.tensor_copy(floor[:], columns[:, ROW_TILES : ROW_TILES + CALL_TILES])
+
+        v_codes, v_scales = [], []
+        for half in range(S // BANK):
+            scales = keep.tile([P, BANK], U8, name="v_scales%d" % half, align_bytes=64)
+            nc.vector.tensor_copy(scales[:], tab_plane[:].indirect(part_of(clip_list, BANK * half, BANK)))
+            v_scales.append(scales)
+        for half in range(S // BANK):
+            codes = keep.tile([P, BANK], U32, name="v_codes%d" % half, align_bytes=64)
+            nc.vector.tensor_copy(codes[:], tab_tile[:].indirect(part_of(clip_list, BANK * half, BANK)))
+            v_codes.append(codes)
+
+        w1_codes = {}
+
+        def quantise_w1(lo, hi):
+            load = 0 if hi <= W1_LOADS[0][1] else 1
+            first = W1_LOADS[load][0]
+            grouped = keep.tile([P, (hi - lo) * PACK], BF16, name="w1_grouped%d" % lo, align_bytes=64)
+            nc.scalar.copy(
+                out=grouped[:].rearrange("p (c i j) -> p c j i", i=4, j=PACK),
+                in_=w1_raw[load][:, :, lo - first : hi - first].rearrange("p j (c i) -> p c j i", i=4),
+            )
+            codes = keep.tile([P, hi - lo], U32, name="w1_codes%d" % lo, align_bytes=64)
+            scales = keep.tile([P, hi - lo], U8, name="w1_scales%d" % lo, align_bytes=64)
+            nc.vector.quantize_mx(out=codes[:].bitcast(FP8X4), scales=scales[:], in_=grouped[:])
+            for c0 in range(lo, hi, P):
+                w1_codes[c0 // P] = (codes[:, c0 - lo : c0 - lo + P], scales[:, c0 - lo : c0 - lo + P])
+
+        factors = {}
+
+        def phases(b):
+            if b == LAST:
+                wave = ring.tile([P, S], F32, name="wave_last", tag="wave_last", align_bytes=64)
+            else:
+                wave = ring.tile([P, S], F32, name="wave", tag="wave", bufs=3)
+            unit = ring.tile([P, S], F32, name="unit", tag="unit", bufs=2)
+            codes, scales = w1_codes[b]
+            folded = ring.tile([P, S], F32, name="folded", tag="folded", bufs=2)
+            for half in range(S // BANK):
+                cols = slice(BANK * half, BANK * (half + 1))
+                acc = banks[half]
+                nc.tensor.matmul_mx(
+                    out=acc[:],
+                    lhsT=w4_tile[:, 2 * P * b : 2 * P * (b + 1)].bitcast(FP4X4), lhsT_scale=w4_plane[:, P * b : P * (b + 1)],
+                    rhs=v_codes[half][:].bitcast(FP8X4), rhs_scale=v_scales[half][:], start=True, stop=False,
+                )
+                nc.tensor.matmul_mx(
+                    out=acc[:], lhsT=codes.bitcast(FP8X4), lhsT_scale=scales,
+                    rhs=v_codes[half][:].bitcast(FP8X4), rhs_scale=v_scales[half][:], start=False, stop=True,
+                )
+                nc.scalar.activation(out=folded[:, cols], in_=acc[:], func=ACT.Abs, bias=-math.pi / 4)
+                if b == 0:
+                    nc.scalar.activation(out=unit[:, cols], in_=folded[:, cols], func=ACT.Sin, scale=-1.0, bias=math.pi / 2)
+                    nc.vector.tensor_scalar(wave[:, cols], unit[:, cols], amp_gain[:, b : b + 1], None, ALU.mult)
+            if b != 0:
+                nc.scalar.activation(out=unit[:], in_=folded[:], func=ACT.Sin, scale=-1.0, bias=math.pi / 2)
+                nc.scalar.activation(out=wave[:], in_=unit[:], func=ACT.Copy, scale=amp_gain[:, b : b + 1])
+            factors[b] = wave
+
+        def scatter(b):
+            wave = factors[b]
+            width = BANK if b == 0 else S
+            for first in range(0, S, width):
+                cols = slice(first, first + width)
+                nc.vector.tensor_tensor(
+                    pages[b][:].indirect(part_of(place_list, first, width)), wave[:, cols], wgs_tile[:, cols], ALU.mult
+                )
+
+        turned = {}
+
+        def turn_page(b, q):
+            a, w = divmod(b, PACK)
+            if w == 0:
+                turned[a, q] = keep.tile([P, 4 * P * PACK], BF16, name="turned%d_%d" % (a, q), align_bytes=64)
+            bank = banks[q if b == LAST else q % 2]
+            for i in range(4):
+                c0 = BANK * q + P * i
+                nc.tensor.transpose(bank[:, P * i : P * (i + 1)], pages[b][:, c0 : c0 + P], ident[:])
+            nc.scalar.copy(
+                out=turned[a, q][:].rearrange("c (i u p e) -> c i u p e", i=4, u=2, e=2)[:, :, :, 32 * w : 32 * (w + 1), :],
+                in_=bank[:].rearrange("c (i p u e) -> c i u p e", i=4, u=2, e=2),
+            )
+
+        woven = {}
+
+        def turn_back(a, q):
+            if a == 0:
+                tile = keep.tile([P, 2 * BANK], F32, name="woven0_%d" % q, align_bytes=64)
+            else:
+                tile = ring.tile([P, 2 * BANK], F32, name="woven1", bufs=3, align_bytes=64)
+            pairs = turned[a, q][:].bitcast(F32)
+            for k in range(2):
+                bank = banks[4 + (2 * q + k) % 4]
+                for j in range(4):
+                    c0 = BANK * k + P * j
+                    nc.tensor.transpose(bank[:, P * j : P * (j + 1)], pairs[:, c0 : c0 + P], ident[:])
+                nc.scalar.copy(
+                    out=tile[:, BANK * k : BANK * (k + 1)].rearrange("p (i c u) -> p i c u", i=2, u=2),
+                    in_=bank[:].rearrange("p (i u c) -> p i c u", i=2, u=2),
+                )
+            woven[a, q] = tile
+
+        page_codes = {}
+
+        def quantise_page(a, q, scales):
+            codes = keep.tile([P, BANK], U32, name="page_codes%d_%d" % (a, q), align_bytes=64)
+            nc.vector.quantize_mx(out=codes[:].bitcast(FP8X4), scales=scales, in_=woven[a, q][:].bitcast(BF16))
+            page_codes[a, q] = (codes, scales)
+
+        for b in range(AHEAD):
+            quantise_w1(*W1_GROUPS[b])
+        for b in range(AHEAD):
+            phases(b)
+        for group in W1_GROUPS[AHEAD:]:
+            quantise_w1(*group)
+        for b in range(ROW_TILES):
+            if b + AHEAD < ROW_TILES:
+                phases(b + AHEAD)
+            scatter(b)
+            if b == LAST:
+                break
+            for q in range(CHUNKS):
+                turn_page(b, q)
+            if b + 4 < ROW_TILES:
+                load_page(b + 4)
+            if b >= LAST - 2:
+                for q in range(2):
+                    turn_back(0, 2 * (b - LAST + 2) + q)
+
+        call_codes = ring.tile([P, PASSES * S2], U32, name="call_codes", tag="wave_last", align_bytes=64)
+        late_scales = ring.tile([P, T2], U8, name="late_scales", tag="wgs", align_bytes=64)
+        call_scales = keep.tile([P, S2], U8, name="call_scales", align_bytes=64)
+        nc.vector.tensor_copy(call_scales[:], tab2_plane[:].indirect(call_list[:]))
+        for a in range(PASSES):
+            nc.vector.tensor_copy(call_codes[:, S2 * a : S2 * (a + 1)], tab2_tiles[a][:].indirect(call_list[:]))
+        for q in range(CHUNKS):
+            quantise_page(0, q, late_scales[:, BANK * q : BANK * (q + 1)])
+        for q in range(CHUNKS):
+            turn_page(LAST, q)
+        for q in range(CHUNKS):
+            turn_back(1, q)
+            last_scales = keep.tile([P, BANK], U8, name="page_scales1_%d" % q, align_bytes=64)
+            quantise_page(1, q, last_scales[:])
+
+        def scores(n):
+            e = ring.tile([P, T2], F32, name="e", tag="rows", bufs=4)
+            for q in range(CHUNKS):
+                acc = banks[(CHUNKS * n + q) % 8]
+                for a in range(PASSES):
+                    codes, scales = page_codes[a, q]
+                    nc.tensor.matmul_mx(
+                        out=acc[:],
+                        lhsT=call_codes[:, S2 * a + P * n : S2 * a + P * (n + 1)].bitcast(FP8X4),
+                        lhsT_scale=call_scales[4 * a : P, P * n : P * (n + 1)],
+                        rhs=codes[:].bitcast(FP8X4), rhs_scale=scales, start=(a == 0), stop=(a == PASSES - 1),
+                    )
+                nc.scalar.copy(out=e[:, BANK * q : BANK * (q + 1)], in_=acc[:])
+            return e
+
+        def finish(n, e):
+            width = BANK if n == CALL_TILES - 1 else PICKS
+            for first in range(0, PICKS, width):
+                picked = ring.tile([P, width], F32, name="picked", tag="wave", bufs=3)
+                nc.vector.tensor_copy(picked[:], e[:].indirect(part_of(read_list, first, width)))
+                nc.vector.tensor_scalar(picked[:], picked[:], floor[:, n : n + 1], None, ALU.max)
+                result = ring.tile([P, width], F32, name="result", tag="result", bufs=3)
+                nc.scalar.activation(out=result[:], in_=picked[:], func=ACT.Square)
+                nc.sync.dma_start(out=out[P * n : P * (n + 1), first : first + width], in_=result[:])
+
+        score_tiles = [scores(n) for n in range(CALL_TILES)]
+        for n in range(CALL_TILES):
+            finish(n, score_tiles[n])

@@ -30,6 +30,8 @@ LAST = ROW_TILES - 1
 W1_LOADS = ((0, 256), (256, 1024))
 W1_GROUPS = ((0, 128), (128, 256), (256, 512), (512, 1024))
 AHEAD = 2
+BOUND_ON_SCALAR = 2
+FIRST_PIECES = ((0, 256), (256, 256), (512, 512))
 
 
 def tile_list_birdsong_retrieval_kernel(
@@ -41,6 +43,7 @@ def tile_list_birdsong_retrieval_kernel(
         lists = ctx.enter_context(tc.tile_pool(name="lists", bufs=1))
         keep = ctx.enter_context(tc.tile_pool(name="keep", bufs=1))
         ring = ctx.enter_context(tc.tile_pool(name="ring", bufs=1))
+        slab = ctx.enter_context(tc.tile_pool(name="slab", bufs=1))
         psum = ctx.enter_context(tc.psum_pool(name="psum", bufs=1))
 
         def load_list(name, source):
@@ -74,8 +77,9 @@ def tile_list_birdsong_retrieval_kernel(
         nc.gpsimd.memset(vectors[:], 0.0)
         ident = keep.tile([P, P], F32, name="ident")
         make_identity(nc, ident[:])
-        nc.gpsimd.dma_start(out=vectors[0:ROW_TILES, :], in_=gain.rearrange("(b p) -> b p", p=P))
-        nc.gpsimd.dma_start(out=vectors[ROW_TILES : ROW_TILES + CALL_TILES, :], in_=low.rearrange("(n p) -> n p", p=P))
+        nc.gpsimd.dma_start(out=vectors[0:PACK, :], in_=gain[0 : H // 2].rearrange("(b p) -> b p", p=P))
+        low_rows = keep.tile([P, P], F32, name="low_rows")
+        nc.gpsimd.memset(low_rows[:], 0.0)
 
         w1_raw = []
 
@@ -89,7 +93,11 @@ def tile_list_birdsong_retrieval_kernel(
 
         def load_page(b):
             page = ring.tile([P, T2], F32, name="page", tag="rows", bufs=4)
-            nc.sync.dma_start(out=page[:], in_=page0[P * b : P * (b + 1), :])
+            if b < PACK:
+                rows = page0[P * b : P * (b + 1), :]
+            else:
+                rows = page0[H // 2 :, :].rearrange("(p t) c -> p t c", t=PACK)[:, b - PACK, :]
+            nc.sync.dma_start(out=page[:], in_=rows)
             pages.append(page)
 
         clip_list = load_list("clip_list", offs)
@@ -97,33 +105,25 @@ def tile_list_birdsong_retrieval_kernel(
         nc.sync.dma_start(out=w4_tile[:].bitcast(I32), in_=w4_words[0].bitcast(I32))
         load_w1(0)
         load_scale_rows(nc.sync, tab_plane, tab_scales)
-        tab_tile = keep.tile([P, T], U32, name="tab_tile", align_bytes=64)
+        tab_tile = slab.tile([P, T], U32, name="tab_tile", align_bytes=64, offset=0)
         nc.sync.dma_start(out=tab_tile[:].bitcast(I32), in_=tab_words[0].rearrange("p t i -> p (t i)").bitcast(I32))
         load_scale_rows(nc.sync, w4_plane, w4_scales)
-        wgs_tile = ring.tile([P, S], F32, name="wgs_tile", tag="wgs", align_bytes=64)
+        wgs_tile = keep.tile([P, S], F32, name="wgs_tile")
         nc.sync.dma_start(out=wgs_tile[:], in_=wgs)
         place_list = load_list("place_list", offs3)
         load_page(0)
         load_w1(1)
         load_page(1)
+        gain_upper = keep.tile([P, PACK], F32, name="gain_upper")
+        nc.sync.dma_start(out=gain_upper[:], in_=gain[H // 2 :].rearrange("(p t) -> p t", t=PACK))
+        nc.sync.dma_start(out=low_rows[0:CALL_TILES, :], in_=low.rearrange("(n p) -> n p", p=P))
         load_page(2)
         load_page(3)
-        tab2_tiles = []
-        for a in range(PASSES):
-            words = keep.tile([P, T3], U32, name="tab2_tile%d" % a, align_bytes=64)
-            nc.sync.dma_start(out=words[:].bitcast(I32), in_=tab2_words[a].rearrange("p t i -> p (t i)").bitcast(I32))
-            tab2_tiles.append(words)
-        load_scale_rows(nc.sync, tab2_plane, tab2_scales)
-        call_list = load_list("call_list", offs2)
-        read_list = load_list("read_list", offs4)
-
         banks = [psum.tile([P, BANK], F32, name="bank%d" % i) for i in range(8)]
         columns = banks[7]
         nc.tensor.transpose(columns[:, 0:P], vectors[:], ident[:])
         amp_gain = keep.tile([P, ROW_TILES], F32, name="amp_gain")
-        nc.vector.tensor_scalar(amp_gain[:], columns[:, 0:ROW_TILES], half_amp[:], 2.0, ALU.mult, ALU.mult)
-        floor = keep.tile([P, CALL_TILES], F32, name="floor")
-        nc.vector.tensor_copy(floor[:], columns[:, ROW_TILES : ROW_TILES + CALL_TILES])
+        nc.vector.tensor_scalar(amp_gain[:, 0:PACK], columns[:, 0:PACK], half_amp[:], 2.0, ALU.mult, ALU.mult)
 
         v_codes, v_scales = [], []
         for half in range(S // BANK):
@@ -135,14 +135,27 @@ def tile_list_birdsong_retrieval_kernel(
             nc.vector.tensor_copy(codes[:], tab_tile[:].indirect(part_of(clip_list, BANK * half, BANK)))
             v_codes.append(codes)
 
+        wgs_upper = slab.tile([P, PACK * S], F32, name="wgs_upper", align_bytes=64, offset=0)
+        for quad in range(4):
+            nc.sync.dma_start(out=wgs_upper[32 * quad : 32 * (quad + 1), :], in_=wgs.rearrange("(m t) j -> m (t j)", t=PACK))
+        tab2_tiles = []
+        for a in range(PASSES):
+            words = keep.tile([P, T3], U32, name="tab2_tile%d" % a, align_bytes=64)
+            nc.sync.dma_start(out=words[:].bitcast(I32), in_=tab2_words[a].rearrange("p t i -> p (t i)").bitcast(I32))
+            tab2_tiles.append(words)
+        load_scale_rows(nc.sync, tab2_plane, tab2_scales)
+        call_list = load_list("call_list", offs2)
+        read_list = load_list("read_list", offs4)
+
         w1_codes = {}
 
         def quantise_w1(lo, hi):
             load = 0 if hi <= W1_LOADS[0][1] else 1
             first = W1_LOADS[load][0]
             grouped = keep.tile([P, (hi - lo) * PACK], BF16, name="w1_grouped%d" % lo, align_bytes=64)
+            order = "p (c i j) -> p c j i" if lo < H // 2 else "p (i c j) -> p c j i"
             nc.scalar.copy(
-                out=grouped[:].rearrange("p (c i j) -> p c j i", i=4, j=PACK),
+                out=grouped[:].rearrange(order, i=4, j=PACK),
                 in_=w1_raw[load][:, :, lo - first : hi - first].rearrange("p j (c i) -> p c j i", i=4),
             )
             codes = keep.tile([P, hi - lo], U32, name="w1_codes%d" % lo, align_bytes=64)
@@ -151,147 +164,255 @@ def tile_list_birdsong_retrieval_kernel(
             for c0 in range(lo, hi, P):
                 w1_codes[c0 // P] = (codes[:, c0 - lo : c0 - lo + P], scales[:, c0 - lo : c0 - lo + P])
 
+        w4_upper = keep.tile([P, H], U8, name="w4_upper", align_bytes=64)
+        w4_upper_plane = keep.tile([P, H // 2], U8, name="w4_upper_plane", align_bytes=64)
+
+        def order_upper_w4():
+            nc.vector.tensor_copy(
+                out=w4_upper[:].bitcast(U16).rearrange("p (t m) -> p m t", t=PACK),
+                in_=w4_tile[:, H:].bitcast(U16).rearrange("p (m t) -> p m t", t=PACK),
+            )
+            nc.vector.tensor_copy(
+                out=w4_upper_plane[:].rearrange("p (t m) -> p m t", t=PACK),
+                in_=w4_plane[:, H // 2 :].rearrange("p (m t) -> p m t", t=PACK),
+            )
+
         factors = {}
 
         def phases(b):
-            if b == LAST:
-                wave = ring.tile([P, S], F32, name="wave_last", tag="wave_last", align_bytes=64)
-            else:
-                wave = ring.tile([P, S], F32, name="wave", tag="wave", bufs=3)
-            unit = ring.tile([P, S], F32, name="unit", tag="unit", bufs=2)
+            wave = ring.tile([P, S], F32, name="wave", tag="wave", bufs=4)
             codes, scales = w1_codes[b]
-            folded = ring.tile([P, S], F32, name="folded", tag="folded", bufs=2)
-            for half in range(S // BANK):
-                cols = slice(BANK * half, BANK * (half + 1))
-                acc = banks[half]
-                nc.tensor.matmul_mx(
-                    out=acc[:],
-                    lhsT=w4_tile[:, 2 * P * b : 2 * P * (b + 1)].bitcast(FP4X4), lhsT_scale=w4_plane[:, P * b : P * (b + 1)],
-                    rhs=v_codes[half][:].bitcast(FP8X4), rhs_scale=v_scales[half][:], start=True, stop=False,
-                )
-                nc.tensor.matmul_mx(
-                    out=acc[:], lhsT=codes.bitcast(FP8X4), lhsT_scale=scales,
-                    rhs=v_codes[half][:].bitcast(FP8X4), rhs_scale=v_scales[half][:], start=False, stop=True,
-                )
-                nc.scalar.activation(out=folded[:, cols], in_=acc[:], func=ACT.Abs, bias=-math.pi / 4)
-                if b == 0:
-                    nc.scalar.activation(out=unit[:, cols], in_=folded[:, cols], func=ACT.Sin, scale=-1.0, bias=math.pi / 2)
-                    nc.vector.tensor_scalar(wave[:, cols], unit[:, cols], amp_gain[:, b : b + 1], None, ALU.mult)
-            if b != 0:
-                nc.scalar.activation(out=unit[:], in_=folded[:], func=ACT.Sin, scale=-1.0, bias=math.pi / 2)
-                nc.scalar.activation(out=wave[:], in_=unit[:], func=ACT.Copy, scale=amp_gain[:, b : b + 1])
+            if b < PACK:
+                w4_codes, w4_bytes = w4_tile[:, 2 * P * b : 2 * P * (b + 1)], w4_plane[:, P * b : P * (b + 1)]
+            else:
+                t = b - PACK
+                w4_codes, w4_bytes = w4_upper[:, 2 * P * t : 2 * P * (t + 1)], w4_upper_plane[:, P * t : P * (t + 1)]
+
+            def products(acc, first, width):
+                half, c0 = divmod(first, BANK)
+                step = BANK if width == BANK else P
+                for c in range(0, width, step):
+                    cols = slice(c0 + c, c0 + c + step)
+                    moving, moving_scale = v_codes[half][:, cols].bitcast(FP8X4), v_scales[half][:, cols]
+                    nc.tensor.matmul_mx(
+                        out=acc[:, c : c + step], lhsT=w4_codes.bitcast(FP4X4), lhsT_scale=w4_bytes,
+                        rhs=moving, rhs_scale=moving_scale, start=True, stop=False,
+                    )
+                    nc.tensor.matmul_mx(
+                        out=acc[:, c : c + step], lhsT=codes.bitcast(FP8X4), lhsT_scale=scales,
+                        rhs=moving, rhs_scale=moving_scale, start=False, stop=True,
+                    )
+
+            def fold(folded, acc):
+                nc.scalar.activation(out=folded, in_=acc, func=ACT.Abs, bias=-math.pi / 4)
+
+            def cosine(unit, folded):
+                nc.scalar.activation(out=unit, in_=folded, func=ACT.Sin, scale=-1.0, bias=math.pi / 2)
+
+            def amplify(result, unit):
+                nc.scalar.activation(out=result, in_=unit, func=ACT.Copy, scale=amp_gain[:, b : b + 1])
+
+            if b == 0:
+                folded = ring.tile([P, S], F32, name="folded", tag="work", bufs=4)
+                for (first, width), acc in zip(FIRST_PIECES, (banks[2], banks[0], banks[1])):
+                    cols = slice(first, first + width)
+                    products(acc, first, width)
+                    fold(folded[:, cols], acc[:, 0:width])
+                    cosine(wave[:, cols], folded[:, cols])
+            elif b == LAST:
+                for half in range(S // BANK):
+                    folded = ring.tile([P, BANK], F32, name="folded_half", tag="pairs%d" % (2 * half), align_bytes=64)
+                    unit = ring.tile([P, BANK], F32, name="unit_half", tag="pairs%d" % (2 * half + 1), align_bytes=64)
+                    products(banks[half], BANK * half, BANK)
+                    fold(folded[:], banks[half][:])
+                    cosine(unit[:], folded[:])
+                    amplify(wave[:, BANK * half : BANK * (half + 1)], unit[:])
+            else:
+                folded = ring.tile([P, S], F32, name="folded", tag="work", bufs=4)
+                unit = ring.tile([P, S], F32, name="unit", tag="work", bufs=4)
+                for half in range(S // BANK):
+                    products(banks[half], BANK * half, BANK)
+                    fold(folded[:, BANK * half : BANK * (half + 1)], banks[half][:])
+                cosine(unit[:], folded[:])
+                amplify(wave[:], unit[:])
             factors[b] = wave
 
         def scatter(b):
             wave = factors[b]
-            width = BANK if b == 0 else S
-            for first in range(0, S, width):
+            if b == 0:
+                weights = first_weights[:]
+            elif b < PACK:
+                weights = wgs_tile[:]
+            else:
+                weights = wgs_upper[:, S * (b - PACK) : S * (b - PACK + 1)]
+            for first, width in FIRST_PIECES if b == 0 else ((0, S),):
                 cols = slice(first, first + width)
                 nc.vector.tensor_tensor(
-                    pages[b][:].indirect(part_of(place_list, first, width)), wave[:, cols], wgs_tile[:, cols], ALU.mult
+                    pages[b][:].indirect(part_of(place_list, first, width)), wave[:, cols], weights[:, cols], ALU.mult
                 )
 
         turned = {}
 
         def turn_page(b, q):
-            a, w = divmod(b, PACK)
-            if w == 0:
-                turned[a, q] = keep.tile([P, 4 * P * PACK], BF16, name="turned%d_%d" % (a, q), align_bytes=64)
-            bank = banks[q if b == LAST else q % 2]
+            if b == 0:
+                turned[q] = keep.tile([P, 4 * P * PACK], BF16, name="turned%d" % q, align_bytes=64)
+            bank = banks[q % 2]
             for i in range(4):
                 c0 = BANK * q + P * i
                 nc.tensor.transpose(bank[:, P * i : P * (i + 1)], pages[b][:, c0 : c0 + P], ident[:])
             nc.scalar.copy(
-                out=turned[a, q][:].rearrange("c (i u p e) -> c i u p e", i=4, u=2, e=2)[:, :, :, 32 * w : 32 * (w + 1), :],
+                out=turned[q][:].rearrange("c (i u p e) -> c i u p e", i=4, u=2, e=2)[:, :, :, 32 * b : 32 * (b + 1), :],
                 in_=bank[:].rearrange("c (i p u e) -> c i u p e", i=4, u=2, e=2),
             )
 
         woven = {}
 
-        def turn_back(a, q):
-            if a == 0:
-                tile = keep.tile([P, 2 * BANK], F32, name="woven0_%d" % q, align_bytes=64)
-            else:
-                tile = ring.tile([P, 2 * BANK], F32, name="woven1", bufs=3, align_bytes=64)
-            pairs = turned[a, q][:].bitcast(F32)
+        def turn_back(q):
+            tile = keep.tile([P, 2 * BANK], F32, name="woven0_%d" % q, align_bytes=64)
+            words = turned[q][:].bitcast(F32)
             for k in range(2):
                 bank = banks[4 + (2 * q + k) % 4]
                 for j in range(4):
                     c0 = BANK * k + P * j
-                    nc.tensor.transpose(bank[:, P * j : P * (j + 1)], pairs[:, c0 : c0 + P], ident[:])
+                    nc.tensor.transpose(bank[:, P * j : P * (j + 1)], words[:, c0 : c0 + P], ident[:])
                 nc.scalar.copy(
                     out=tile[:, BANK * k : BANK * (k + 1)].rearrange("p (i c u) -> p i c u", i=2, u=2),
                     in_=bank[:].rearrange("p (i u c) -> p i c u", i=2, u=2),
                 )
-            woven[a, q] = tile
+            woven[0, q] = tile
+
+        pairs = {}
+
+        def round_page(b, q):
+            u, e = divmod(b - PACK, 2)
+            if b == PACK:
+                pairs[q] = ring.tile([P, PACK * BANK], BF16, name="pairs", tag="pairs%d" % q, align_bytes=64)
+            nc.scalar.copy(
+                out=pairs[q][:].rearrange("p (u c e) -> p u c e", u=2, e=2)[:, u, :, e],
+                in_=pages[b][:, BANK * q : BANK * (q + 1)],
+            )
+
+        def weave(q):
+            tile = keep.tile([P, 2 * BANK], F32, name="woven1_%d" % q, align_bytes=64)
+            copy = nc.scalar.copy if q < CHUNKS // 2 else nc.vector.tensor_copy
+            copy(
+                out=tile[:].rearrange("p (c u) -> p c u", u=2),
+                in_=pairs[q][:].bitcast(F32).rearrange("p (u c) -> p c u", u=2),
+            )
+            woven[1, q] = tile
 
         page_codes = {}
 
         def quantise_page(a, q, scales):
-            codes = keep.tile([P, BANK], U32, name="page_codes%d_%d" % (a, q), align_bytes=64)
+            codes = keep.tile([P, BANK], U32, name="page_codes", tag="codes%d" % (PASSES * q + a), align_bytes=64)
             nc.vector.quantize_mx(out=codes[:].bitcast(FP8X4), scales=scales, in_=woven[a, q][:].bitcast(BF16))
             page_codes[a, q] = (codes, scales)
 
         for b in range(AHEAD):
             quantise_w1(*W1_GROUPS[b])
+        first_weights = ring.tile([P, S], F32, name="first_weights", tag="work", bufs=4)
+        nc.vector.tensor_scalar(first_weights[:], wgs_tile[:], amp_gain[:, 0:1], None, ALU.mult)
         for b in range(AHEAD):
             phases(b)
         for group in W1_GROUPS[AHEAD:]:
             quantise_w1(*group)
-        for b in range(ROW_TILES):
-            if b + AHEAD < ROW_TILES:
-                phases(b + AHEAD)
+        order_upper_w4()
+        nc.vector.tensor_scalar(amp_gain[:, PACK:], gain_upper[:], half_amp[:], 2.0, ALU.mult, ALU.mult)
+        nc.tensor.transpose(banks[6][:, 0:P], low_rows[:], ident[:])
+        floor = keep.tile([P, CALL_TILES], F32, name="floor")
+        nc.scalar.copy(out=floor[:], in_=banks[6][:, 0:CALL_TILES])
+        minus_floor = keep.tile([P, CALL_TILES], F32, name="minus_floor")
+        nc.scalar.activation(out=minus_floor[:], in_=banks[6][:, 0:CALL_TILES], func=ACT.Copy, scale=-1.0)
+        for b in range(PACK):
+            phases(b + AHEAD)
             scatter(b)
-            if b == LAST:
-                break
             for q in range(CHUNKS):
                 turn_page(b, q)
-            if b + 4 < ROW_TILES:
-                load_page(b + 4)
-            if b >= LAST - 2:
-                for q in range(2):
-                    turn_back(0, 2 * (b - LAST + 2) + q)
+            load_page(b + PACK)
+        for b in range(PACK + AHEAD, ROW_TILES):
+            phases(b)
+        for q in range(CHUNKS):
+            turn_back(q)
+        for b in range(PACK, ROW_TILES):
+            scatter(b)
+            if b < LAST:
+                for q in range(CHUNKS):
+                    round_page(b, q)
 
-        call_codes = ring.tile([P, PASSES * S2], U32, name="call_codes", tag="wave_last", align_bytes=64)
-        late_scales = ring.tile([P, T2], U8, name="late_scales", tag="wgs", align_bytes=64)
-        call_scales = keep.tile([P, S2], U8, name="call_scales", align_bytes=64)
-        nc.vector.tensor_copy(call_scales[:], tab2_plane[:].indirect(call_list[:]))
-        for a in range(PASSES):
-            nc.vector.tensor_copy(call_codes[:, S2 * a : S2 * (a + 1)], tab2_tiles[a][:].indirect(call_list[:]))
+        half_calls = S2 // 2
+        call_codes, call_scales = [], []
+
+        def gather_call_scales(tile, half):
+            nc.vector.tensor_copy(tile[:], tab2_plane[:].indirect(part_of(call_list, half_calls * half, half_calls)))
+            call_scales.append(tile)
+
+        def gather_call_words(tile, half, a):
+            nc.vector.tensor_copy(
+                tile[:, half_calls * a : half_calls * (a + 1)],
+                tab2_tiles[a][:].indirect(part_of(call_list, half_calls * half, half_calls)),
+            )
+
+        late_scales = slab.tile([P, T2], U8, name="late_scales", align_bytes=64, offset=4096)
+        gather_call_scales(slab.tile([P, half_calls], U8, name="call_scales0", align_bytes=64, offset=8192), 0)
+        call_codes.append(slab.tile([P, PASSES * half_calls], U32, name="call_codes0", align_bytes=64, offset=0))
+        gather_call_words(call_codes[0], 0, 0)
         for q in range(CHUNKS):
             quantise_page(0, q, late_scales[:, BANK * q : BANK * (q + 1)])
+        gather_call_words(call_codes[0], 0, 1)
         for q in range(CHUNKS):
-            turn_page(LAST, q)
+            round_page(LAST, q)
+            if q < CHUNKS // 2:
+                weave(q)
         for q in range(CHUNKS):
-            turn_back(1, q)
+            if q == CHUNKS // 2:
+                weave(q)
+                weave(q + 1)
             last_scales = keep.tile([P, BANK], U8, name="page_scales1_%d" % q, align_bytes=64)
             quantise_page(1, q, last_scales[:])
+        gather_call_scales(ring.tile([P, half_calls], U8, name="call_scales1", tag="pairs2", align_bytes=64), 1)
+        call_codes.append(ring.tile([P, PASSES * half_calls], U32, name="call_codes1", tag="pairs3", align_bytes=64))
+        for a in range(PASSES):
+            gather_call_words(call_codes[1], 1, a)
+
+        def product(n, q, a):
+            codes, scales = page_codes[a, q]
+            half, c0 = n // 2, P * (n % 2)
+            nc.tensor.matmul_mx(
+                out=banks[(CHUNKS * n + q) % 8][:],
+                lhsT=call_codes[half][:, half_calls * a + c0 : half_calls * a + c0 + P].bitcast(FP8X4),
+                lhsT_scale=call_scales[half][4 * a : P, c0 : c0 + P],
+                rhs=codes[:].bitcast(FP8X4), rhs_scale=scales, start=(a == 0), stop=(a == PASSES - 1),
+            )
 
         def scores(n):
             e = ring.tile([P, T2], F32, name="e", tag="rows", bufs=4)
             for q in range(CHUNKS):
-                acc = banks[(CHUNKS * n + q) % 8]
-                for a in range(PASSES):
-                    codes, scales = page_codes[a, q]
-                    nc.tensor.matmul_mx(
-                        out=acc[:],
-                        lhsT=call_codes[:, S2 * a + P * n : S2 * a + P * (n + 1)].bitcast(FP8X4),
-                        lhsT_scale=call_scales[4 * a : P, P * n : P * (n + 1)],
-                        rhs=codes[:].bitcast(FP8X4), rhs_scale=scales, start=(a == 0), stop=(a == PASSES - 1),
-                    )
-                nc.scalar.copy(out=e[:, BANK * q : BANK * (q + 1)], in_=acc[:])
+                if n >= 2:
+                    product(n, q, 0)
+                product(n, q, 1)
+                nc.scalar.copy(out=e[:, BANK * q : BANK * (q + 1)], in_=banks[(CHUNKS * n + q) % 8][:])
             return e
 
+        spare_tags = list(range(PASSES * CHUNKS))
+
         def finish(n, e):
-            width = BANK if n == CALL_TILES - 1 else PICKS
-            for first in range(0, PICKS, width):
-                picked = ring.tile([P, width], F32, name="picked", tag="wave", bufs=3)
+            cuts = (0, 512, 768, 1024) if n == CALL_TILES - 1 else (0, PICKS)
+            for first, end in zip(cuts, cuts[1:]):
+                width = end - first
+                picked = ring.tile([P, width], F32, name="picked", tag="wave", bufs=4)
                 nc.vector.tensor_copy(picked[:], e[:].indirect(part_of(read_list, first, width)))
-                nc.vector.tensor_scalar(picked[:], picked[:], floor[:, n : n + 1], None, ALU.max)
-                result = ring.tile([P, width], F32, name="result", tag="result", bufs=3)
-                nc.scalar.activation(out=result[:], in_=picked[:], func=ACT.Square)
+                result = keep.tile([P, width], F32, name="result", tag="codes%d" % spare_tags.pop(), align_bytes=64)
+                if n < BOUND_ON_SCALAR:
+                    nc.scalar.activation(out=result[:], in_=picked[:], func=ACT.Relu, bias=minus_floor[:, n : n + 1])
+                    nc.scalar.activation(out=result[:], in_=result[:], func=ACT.Square, bias=floor[:, n : n + 1])
+                else:
+                    nc.vector.tensor_scalar(picked[:], picked[:], floor[:, n : n + 1], None, ALU.max)
+                    nc.scalar.activation(out=result[:], in_=picked[:], func=ACT.Square)
                 nc.sync.dma_start(out=out[P * n : P * (n + 1), first : first + width], in_=result[:])
 
+        for q in range(CHUNKS):
+            for n in range(2):
+                product(n, q, 0)
         score_tiles = [scores(n) for n in range(CALL_TILES)]
         for n in range(CALL_TILES):
             finish(n, score_tiles[n])

@@ -27,10 +27,11 @@ PASSES = H // (P * PACK)
 CHUNKS = T2 // BANK
 CALL_TILES = S2 // P
 LAST = ROW_TILES - 1
-W1_LOADS = ((0, 256), (256, 1024))
+W1_LOADS = ((0, 128), (128, 256), (256, 1024))
 W1_GROUPS = ((0, 128), (128, 256), (256, 512), (512, 1024))
 AHEAD = 2
-BOUND_ON_SCALAR = 2
+PIECE = 256
+BOUND_ON_SCALAR = 1
 FIRST_PIECES = ((0, 256), (256, 256), (512, 512))
 
 
@@ -44,6 +45,7 @@ def tile_list_birdsong_retrieval_kernel(
         keep = ctx.enter_context(tc.tile_pool(name="keep", bufs=1))
         ring = ctx.enter_context(tc.tile_pool(name="ring", bufs=1))
         slab = ctx.enter_context(tc.tile_pool(name="slab", bufs=1))
+        shelf = ctx.enter_context(tc.tile_pool(name="shelf", bufs=1))
         psum = ctx.enter_context(tc.psum_pool(name="psum", bufs=1))
 
         def load_list(name, source):
@@ -101,18 +103,19 @@ def tile_list_birdsong_retrieval_kernel(
             pages.append(page)
 
         clip_list = load_list("clip_list", offs)
-        w4_tile = keep.tile([P, 2 * H], U8, name="w4_tile", align_bytes=64)
-        nc.sync.dma_start(out=w4_tile[:].bitcast(I32), in_=w4_words[0].bitcast(I32))
+        wgs_tile = shelf.tile([P, S], F32, name="wgs_tile", align_bytes=64, offset=(PACK - 1) * 4 * S)
+        nc.sync.dma_start(out=wgs_tile[:], in_=wgs)
         load_w1(0)
         load_scale_rows(nc.sync, tab_plane, tab_scales)
         tab_tile = slab.tile([P, T], U32, name="tab_tile", align_bytes=64, offset=0)
         nc.sync.dma_start(out=tab_tile[:].bitcast(I32), in_=tab_words[0].rearrange("p t i -> p (t i)").bitcast(I32))
+        w4_tile = keep.tile([P, 2 * H], U8, name="w4_tile", align_bytes=64)
+        nc.sync.dma_start(out=w4_tile[:].bitcast(I32), in_=w4_words[0].bitcast(I32))
         load_scale_rows(nc.sync, w4_plane, w4_scales)
-        wgs_tile = keep.tile([P, S], F32, name="wgs_tile")
-        nc.sync.dma_start(out=wgs_tile[:], in_=wgs)
-        place_list = load_list("place_list", offs3)
-        load_page(0)
         load_w1(1)
+        load_page(0)
+        place_list = load_list("place_list", offs3)
+        load_w1(2)
         load_page(1)
         gain_upper = keep.tile([P, PACK], F32, name="gain_upper")
         nc.sync.dma_start(out=gain_upper[:], in_=gain[H // 2 :].rearrange("(p t) -> p t", t=PACK))
@@ -125,32 +128,27 @@ def tile_list_birdsong_retrieval_kernel(
         amp_gain = keep.tile([P, ROW_TILES], F32, name="amp_gain")
         nc.vector.tensor_scalar(amp_gain[:, 0:PACK], columns[:, 0:PACK], half_amp[:], 2.0, ALU.mult, ALU.mult)
 
+        lower_weights = [shelf.tile([P, S], F32, name="weights%d" % b, align_bytes=64, offset=4 * S * b) for b in range(PACK - 1)] + [wgs_tile]
+
         v_codes, v_scales = [], []
         for half in range(S // BANK):
             scales = keep.tile([P, BANK], U8, name="v_scales%d" % half, align_bytes=64)
             nc.vector.tensor_copy(scales[:], tab_plane[:].indirect(part_of(clip_list, BANK * half, BANK)))
             v_scales.append(scales)
-        for half in range(S // BANK):
+        for b in range(PACK):
+            nc.vector.tensor_scalar(lower_weights[b][:], wgs_tile[:], amp_gain[:, b : b + 1], None, ALU.mult)
+
+        def gather_clip_words(half):
             codes = keep.tile([P, BANK], U32, name="v_codes%d" % half, align_bytes=64)
             nc.vector.tensor_copy(codes[:], tab_tile[:].indirect(part_of(clip_list, BANK * half, BANK)))
             v_codes.append(codes)
 
-        wgs_upper = slab.tile([P, PACK * S], F32, name="wgs_upper", align_bytes=64, offset=0)
-        for quad in range(4):
-            nc.sync.dma_start(out=wgs_upper[32 * quad : 32 * (quad + 1), :], in_=wgs.rearrange("(m t) j -> m (t j)", t=PACK))
-        tab2_tiles = []
-        for a in range(PASSES):
-            words = keep.tile([P, T3], U32, name="tab2_tile%d" % a, align_bytes=64)
-            nc.sync.dma_start(out=words[:].bitcast(I32), in_=tab2_words[a].rearrange("p t i -> p (t i)").bitcast(I32))
-            tab2_tiles.append(words)
-        load_scale_rows(nc.sync, tab2_plane, tab2_scales)
-        call_list = load_list("call_list", offs2)
-        read_list = load_list("read_list", offs4)
+        gather_clip_words(0)
 
         w1_codes = {}
 
         def quantise_w1(lo, hi):
-            load = 0 if hi <= W1_LOADS[0][1] else 1
+            load = min(lo // P, len(W1_LOADS) - 1)
             first = W1_LOADS[load][0]
             grouped = keep.tile([P, (hi - lo) * PACK], BF16, name="w1_grouped%d" % lo, align_bytes=64)
             order = "p (c i j) -> p c j i" if lo < H // 2 else "p (i c j) -> p c j i"
@@ -188,23 +186,21 @@ def tile_list_birdsong_retrieval_kernel(
                 t = b - PACK
                 w4_codes, w4_bytes = w4_upper[:, 2 * P * t : 2 * P * (t + 1)], w4_upper_plane[:, P * t : P * (t + 1)]
 
-            def products(acc, first, width):
-                half, c0 = divmod(first, BANK)
-                step = BANK if width == BANK else P
-                for c in range(0, width, step):
-                    cols = slice(c0 + c, c0 + c + step)
+            def fold(folded, piece):
+                half, c0 = divmod(PIECE * piece, BANK)
+                acc = banks[piece]
+                for c in range(0, PIECE, P):
+                    cols = slice(c0 + c, c0 + c + P)
                     moving, moving_scale = v_codes[half][:, cols].bitcast(FP8X4), v_scales[half][:, cols]
                     nc.tensor.matmul_mx(
-                        out=acc[:, c : c + step], lhsT=w4_codes.bitcast(FP4X4), lhsT_scale=w4_bytes,
+                        out=acc[:, c : c + P], lhsT=w4_codes.bitcast(FP4X4), lhsT_scale=w4_bytes,
                         rhs=moving, rhs_scale=moving_scale, start=True, stop=False,
                     )
                     nc.tensor.matmul_mx(
-                        out=acc[:, c : c + step], lhsT=codes.bitcast(FP8X4), lhsT_scale=scales,
+                        out=acc[:, c : c + P], lhsT=codes.bitcast(FP8X4), lhsT_scale=scales,
                         rhs=moving, rhs_scale=moving_scale, start=False, stop=True,
                     )
-
-            def fold(folded, acc):
-                nc.scalar.activation(out=folded, in_=acc, func=ACT.Abs, bias=-math.pi / 4)
+                nc.scalar.activation(out=folded, in_=acc[:, 0:PIECE], func=ACT.Abs, bias=-math.pi / 4)
 
             def cosine(unit, folded):
                 nc.scalar.activation(out=unit, in_=folded, func=ACT.Sin, scale=-1.0, bias=math.pi / 2)
@@ -213,36 +209,35 @@ def tile_list_birdsong_retrieval_kernel(
                 nc.scalar.activation(out=result, in_=unit, func=ACT.Copy, scale=amp_gain[:, b : b + 1])
 
             if b == 0:
-                folded = ring.tile([P, S], F32, name="folded", tag="work", bufs=4)
-                for (first, width), acc in zip(FIRST_PIECES, (banks[2], banks[0], banks[1])):
-                    cols = slice(first, first + width)
-                    products(acc, first, width)
-                    fold(folded[:, cols], acc[:, 0:width])
-                    cosine(wave[:, cols], folded[:, cols])
+                folded = ring.tile([P, S], F32, name="folded", tag="work", bufs=3)
+                for first, width in FIRST_PIECES:
+                    for c in range(first, first + width, PIECE):
+                        fold(folded[:, c : c + PIECE], c // PIECE)
+                    cosine(wave[:, first : first + width], folded[:, first : first + width])
             elif b == LAST:
                 for half in range(S // BANK):
                     folded = ring.tile([P, BANK], F32, name="folded_half", tag="pairs%d" % (2 * half), align_bytes=64)
                     unit = ring.tile([P, BANK], F32, name="unit_half", tag="pairs%d" % (2 * half + 1), align_bytes=64)
-                    products(banks[half], BANK * half, BANK)
-                    fold(folded[:], banks[half][:])
+                    for c in range(0, BANK, PIECE):
+                        fold(folded[:, c : c + PIECE], (BANK * half + c) // PIECE)
                     cosine(unit[:], folded[:])
                     amplify(wave[:, BANK * half : BANK * (half + 1)], unit[:])
             else:
-                folded = ring.tile([P, S], F32, name="folded", tag="work", bufs=4)
-                unit = ring.tile([P, S], F32, name="unit", tag="work", bufs=4)
-                for half in range(S // BANK):
-                    products(banks[half], BANK * half, BANK)
-                    fold(folded[:, BANK * half : BANK * (half + 1)], banks[half][:])
-                cosine(unit[:], folded[:])
-                amplify(wave[:], unit[:])
+                folded = ring.tile([P, S], F32, name="folded", tag="work", bufs=3)
+                for c in range(0, S, PIECE):
+                    fold(folded[:, c : c + PIECE], c // PIECE)
+                if b < PACK:
+                    cosine(wave[:], folded[:])
+                else:
+                    unit = ring.tile([P, S], F32, name="unit", tag="work", bufs=3)
+                    cosine(unit[:], folded[:])
+                    amplify(wave[:], unit[:])
             factors[b] = wave
 
         def scatter(b):
             wave = factors[b]
-            if b == 0:
-                weights = first_weights[:]
-            elif b < PACK:
-                weights = wgs_tile[:]
+            if b < PACK:
+                weights = lower_weights[b][:]
             else:
                 weights = wgs_upper[:, S * (b - PACK) : S * (b - PACK + 1)]
             for first, width in FIRST_PIECES if b == 0 else ((0, S),):
@@ -255,8 +250,8 @@ def tile_list_birdsong_retrieval_kernel(
 
         def turn_page(b, q):
             if b == 0:
-                turned[q] = keep.tile([P, 4 * P * PACK], BF16, name="turned%d" % q, align_bytes=64)
-            bank = banks[q % 2]
+                turned[q] = keep.tile([P, 4 * P * PACK], BF16, name="turned", tag="turned%d" % q, align_bytes=64)
+            bank = banks[q]
             for i in range(4):
                 c0 = BANK * q + P * i
                 nc.tensor.transpose(bank[:, P * i : P * (i + 1)], pages[b][:, c0 : c0 + P], ident[:])
@@ -293,8 +288,8 @@ def tile_list_birdsong_retrieval_kernel(
             )
 
         def weave(q):
-            tile = keep.tile([P, 2 * BANK], F32, name="woven1_%d" % q, align_bytes=64)
-            copy = nc.scalar.copy if q < CHUNKS // 2 else nc.vector.tensor_copy
+            tile = keep.tile([P, 2 * BANK], F32, name="woven1", tag="turned%d" % q, align_bytes=64)
+            copy = nc.scalar.copy if q < CHUNKS - 1 else nc.vector.tensor_copy
             copy(
                 out=tile[:].rearrange("p (c u) -> p c u", u=2),
                 in_=pairs[q][:].bitcast(F32).rearrange("p (u c) -> p c u", u=2),
@@ -308,10 +303,16 @@ def tile_list_birdsong_retrieval_kernel(
             nc.vector.quantize_mx(out=codes[:].bitcast(FP8X4), scales=scales, in_=woven[a, q][:].bitcast(BF16))
             page_codes[a, q] = (codes, scales)
 
-        for b in range(AHEAD):
-            quantise_w1(*W1_GROUPS[b])
-        first_weights = ring.tile([P, S], F32, name="first_weights", tag="work", bufs=4)
-        nc.vector.tensor_scalar(first_weights[:], wgs_tile[:], amp_gain[:, 0:1], None, ALU.mult)
+        quantise_w1(*W1_GROUPS[0])
+        gather_clip_words(1)
+        wgs_upper = slab.tile([P, PACK * S], F32, name="wgs_upper", align_bytes=64, offset=0)
+        for quad in (0, 2, 1, 3):
+            nc.sync.dma_start(out=wgs_upper[32 * quad : 32 * (quad + 1), :], in_=wgs.rearrange("(m t) j -> m (t j)", t=PACK))
+        load_scale_rows(nc.sync, tab2_plane, tab2_scales)
+        call_list = load_list("call_list", offs2)
+        read_list = load_list("read_list", offs4)
+
+        quantise_w1(*W1_GROUPS[1])
         for b in range(AHEAD):
             phases(b)
         for group in W1_GROUPS[AHEAD:]:
@@ -329,6 +330,11 @@ def tile_list_birdsong_retrieval_kernel(
             for q in range(CHUNKS):
                 turn_page(b, q)
             load_page(b + PACK)
+        tab2_tiles = []
+        for a in range(PASSES):
+            words = shelf.tile([P, T3], U32, name="tab2_tile%d" % a, align_bytes=64, offset=4 * T3 * a)
+            nc.sync.dma_start(out=words[:].bitcast(I32), in_=tab2_words[a].rearrange("p t i -> p (t i)").bitcast(I32))
+            tab2_tiles.append(words)
         for b in range(PACK + AHEAD, ROW_TILES):
             phases(b)
         for q in range(CHUNKS):
@@ -359,18 +365,13 @@ def tile_list_birdsong_retrieval_kernel(
         for q in range(CHUNKS):
             quantise_page(0, q, late_scales[:, BANK * q : BANK * (q + 1)])
         gather_call_words(call_codes[0], 0, 1)
-        for q in range(CHUNKS):
+        for q in (0, 1, 3, 2):
             round_page(LAST, q)
-            if q < CHUNKS // 2:
-                weave(q)
-        for q in range(CHUNKS):
-            if q == CHUNKS // 2:
-                weave(q)
-                weave(q + 1)
+            weave(q)
             last_scales = keep.tile([P, BANK], U8, name="page_scales1_%d" % q, align_bytes=64)
             quantise_page(1, q, last_scales[:])
-        gather_call_scales(ring.tile([P, half_calls], U8, name="call_scales1", tag="pairs2", align_bytes=64), 1)
-        call_codes.append(ring.tile([P, PASSES * half_calls], U32, name="call_codes1", tag="pairs3", align_bytes=64))
+        gather_call_scales(ring.tile([P, half_calls], U8, name="call_scales1", tag="pairs3", align_bytes=64), 1)
+        call_codes.append(keep.tile([P, PASSES * half_calls], U32, name="call_codes1", tag="turned2", align_bytes=64))
         for a in range(PASSES):
             gather_call_words(call_codes[1], 1, a)
 

@@ -56,6 +56,11 @@ def tile_list_birdsong_retrieval_kernel(
         def part_of(list_tile, first, count):
             return list_tile[:, first // STRIPE : (first + count) // STRIPE]
 
+        def load_plane(plane, source):
+            rows = source[0].rearrange("(quad r) c -> r quad c", r=4)
+            for r in range(4):
+                nc.sync.dma_start(out=plane[r:P:32, :].bitcast(I32), in_=rows[r].bitcast(I32))
+
         def load_scale_rows(engine, plane, source):
             rows = 4 * source.shape[0]
             for quad in range(4):
@@ -77,9 +82,9 @@ def tile_list_birdsong_retrieval_kernel(
 
         vectors = keep.tile([P, P], F32, name="vectors")
         nc.gpsimd.memset(vectors[:], 0.0)
+        nc.gpsimd.dma_start(out=vectors[0:PACK, :], in_=gain[0 : H // 2].rearrange("(b p) -> b p", p=P))
         ident = keep.tile([P, P], F32, name="ident")
         make_identity(nc, ident[:])
-        nc.gpsimd.dma_start(out=vectors[0:PACK, :], in_=gain[0 : H // 2].rearrange("(b p) -> b p", p=P))
         low_rows = keep.tile([P, P], F32, name="low_rows")
         nc.gpsimd.memset(low_rows[:], 0.0)
 
@@ -106,12 +111,12 @@ def tile_list_birdsong_retrieval_kernel(
         wgs_tile = shelf.tile([P, S], F32, name="wgs_tile", align_bytes=64, offset=(PACK - 1) * 4 * S)
         nc.sync.dma_start(out=wgs_tile[:], in_=wgs)
         load_w1(0)
-        load_scale_rows(nc.sync, tab_plane, tab_scales)
+        load_plane(tab_plane, tab_scales)
         tab_tile = slab.tile([P, T], U32, name="tab_tile", align_bytes=64, offset=0)
         nc.sync.dma_start(out=tab_tile[:].bitcast(I32), in_=tab_words[0].rearrange("p t i -> p (t i)").bitcast(I32))
         w4_tile = keep.tile([P, 2 * H], U8, name="w4_tile", align_bytes=64)
         nc.sync.dma_start(out=w4_tile[:].bitcast(I32), in_=w4_words[0].bitcast(I32))
-        load_scale_rows(nc.sync, w4_plane, w4_scales)
+        load_plane(w4_plane, w4_scales)
         load_w1(1)
         load_page(0)
         place_list = load_list("place_list", offs3)

@@ -31,7 +31,8 @@ W1_LOADS = ((0, 128), (128, 256), (256, 1024))
 W1_GROUPS = ((0, 128), (128, 256), (256, 512), (512, 1024))
 AHEAD = 2
 PIECE = 256
-BOUND_ON_SCALAR = 1
+SQUARE_ON_GPSIMD = 1
+FLOAT_MAX = 3.4028234663852886e38
 FIRST_PIECES = ((0, 256), (256, 256), (512, 512))
 
 
@@ -327,8 +328,6 @@ def tile_list_birdsong_retrieval_kernel(
         nc.tensor.transpose(banks[6][:, 0:P], low_rows[:], ident[:])
         floor = keep.tile([P, CALL_TILES], F32, name="floor")
         nc.scalar.copy(out=floor[:], in_=banks[6][:, 0:CALL_TILES])
-        minus_floor = keep.tile([P, CALL_TILES], F32, name="minus_floor")
-        nc.scalar.activation(out=minus_floor[:], in_=banks[6][:, 0:CALL_TILES], func=ACT.Copy, scale=-1.0)
         for b in range(PACK):
             phases(b + AHEAD)
             scatter(b)
@@ -405,15 +404,21 @@ def tile_list_birdsong_retrieval_kernel(
             cuts = (0, 512, 768, 1024) if n == CALL_TILES - 1 else (0, PICKS)
             for first, end in zip(cuts, cuts[1:]):
                 width = end - first
-                picked = ring.tile([P, width], F32, name="picked", tag="wave", bufs=4)
+                if first == 0:
+                    picked = ring.tile([P, width], F32, name="picked", tag="wave", bufs=4)
+                else:
+                    picked = ring.tile([P, width], F32, name="picked_late", tag="work", bufs=3)
                 nc.vector.tensor_copy(picked[:], e[:].indirect(part_of(read_list, first, width)))
                 result = keep.tile([P, width], F32, name="result", tag="codes%d" % spare_tags.pop(), align_bytes=64)
-                if n < BOUND_ON_SCALAR:
-                    nc.scalar.activation(out=result[:], in_=picked[:], func=ACT.Relu, bias=minus_floor[:, n : n + 1])
-                    nc.scalar.activation(out=result[:], in_=result[:], func=ACT.Square, bias=floor[:, n : n + 1])
-                else:
+                if first > 0:
                     nc.vector.tensor_scalar(picked[:], picked[:], floor[:, n : n + 1], None, ALU.max)
-                    nc.scalar.activation(out=result[:], in_=picked[:], func=ACT.Square)
+                    nc.vector.tensor_tensor(result[:], picked[:], picked[:], ALU.mult)
+                else:
+                    nc.gpsimd.tensor_scalar(picked[:], picked[:], FLOAT_MAX, floor[:, n : n + 1], ALU.min, ALU.max)
+                    if n < SQUARE_ON_GPSIMD:
+                        nc.gpsimd.tensor_tensor(result[:], picked[:], picked[:], ALU.mult)
+                    else:
+                        nc.scalar.activation(out=result[:], in_=picked[:], func=ACT.Square)
                 nc.sync.dma_start(out=out[P * n : P * (n + 1), first : first + width], in_=result[:])
 
         for q in range(CHUNKS):

@@ -27,11 +27,11 @@ PASSES = H // (P * PACK)
 CHUNKS = T2 // BANK
 CALL_TILES = S2 // P
 LAST = ROW_TILES - 1
-W1_LOADS = ((0, 128), (128, 256), (256, 1024))
-W1_GROUPS = ((0, 128), (128, 256), (256, 512), (512, 1024))
+W1_LOADS = ((0, 128), (128, 256), (256, 512), (512, 1024))
 AHEAD = 2
 PIECE = 256
-SQUARE_ON_GPSIMD = 1
+SQUARE_ON_GPSIMD = 2
+VECTOR_WEAVES = 1
 FLOAT_MAX = 3.4028234663852886e38
 FIRST_PIECES = ((0, 256), (256, 256), (512, 512))
 
@@ -47,6 +47,7 @@ def tile_list_birdsong_retrieval_kernel(
         ring = ctx.enter_context(tc.tile_pool(name="ring", bufs=1))
         slab = ctx.enter_context(tc.tile_pool(name="slab", bufs=1))
         shelf = ctx.enter_context(tc.tile_pool(name="shelf", bufs=1))
+        stage = ctx.enter_context(tc.tile_pool(name="stage", bufs=1))
         psum = ctx.enter_context(tc.psum_pool(name="psum", bufs=1))
 
         def load_list(name, source):
@@ -61,14 +62,6 @@ def tile_list_birdsong_retrieval_kernel(
             rows = source[0].rearrange("(quad r) c -> r quad c", r=4)
             for r in range(4):
                 nc.sync.dma_start(out=plane[r:P:32, :].bitcast(I32), in_=rows[r].bitcast(I32))
-
-        def load_scale_rows(engine, plane, source):
-            rows = 4 * source.shape[0]
-            for quad in range(4):
-                engine.dma_start(
-                    out=plane[32 * quad : 32 * quad + rows, :].bitcast(I32),
-                    in_=source[:, 4 * quad : 4 * quad + 4, :].bitcast(I32),
-                )
 
         tab_plane = keep.tile([P, T], U8, name="tab_plane", align_bytes=64)
         nc.vector.memset(tab_plane[:].bitcast(I32), 0)
@@ -86,6 +79,8 @@ def tile_list_birdsong_retrieval_kernel(
         nc.gpsimd.dma_start(out=vectors[0:PACK, :], in_=gain[0 : H // 2].rearrange("(b p) -> b p", p=P))
         ident = keep.tile([P, P], F32, name="ident")
         make_identity(nc, ident[:])
+        call_scales = keep.tile([P, S2], U8, name="call_scales", align_bytes=64)
+        nc.gpsimd.memset(call_scales[:].bitcast(I32), 0)
         low_rows = keep.tile([P, P], F32, name="low_rows")
         nc.gpsimd.memset(low_rows[:], 0.0)
 
@@ -93,7 +88,7 @@ def tile_list_birdsong_retrieval_kernel(
 
         def load_w1(i):
             lo, hi = W1_LOADS[i]
-            raw = keep.tile([P, PACK, hi - lo], F32, name="w1_raw%d" % i)
+            raw = stage.tile([P, PACK, hi - lo], F32, name="w1_raw%d" % i, offset=4 * PACK * lo)
             nc.sync.dma_start(out=raw[:], in_=w1[:, lo:hi].rearrange("(p j) c -> p j c", j=PACK))
             w1_raw.append(raw)
 
@@ -109,20 +104,23 @@ def tile_list_birdsong_retrieval_kernel(
             pages.append(page)
 
         clip_list = load_list("clip_list", offs)
+        call_list = load_list("call_list", offs2)
         wgs_tile = shelf.tile([P, S], F32, name="wgs_tile", align_bytes=64, offset=(PACK - 1) * 4 * S)
         nc.sync.dma_start(out=wgs_tile[:], in_=wgs)
         load_w1(0)
         load_plane(tab_plane, tab_scales)
+        nc.sync.dma_start(out=tab2_plane[0:P:4, :].bitcast(I32), in_=tab2_scales.rearrange("a q t -> (a q) t").bitcast(I32))
         tab_tile = slab.tile([P, T], U32, name="tab_tile", align_bytes=64, offset=0)
         nc.sync.dma_start(out=tab_tile[:].bitcast(I32), in_=tab_words[0].rearrange("p t i -> p (t i)").bitcast(I32))
+        place_list = load_list("place_list", offs3)
         w4_tile = keep.tile([P, 2 * H], U8, name="w4_tile", align_bytes=64)
         nc.sync.dma_start(out=w4_tile[:].bitcast(I32), in_=w4_words[0].bitcast(I32))
         load_plane(w4_plane, w4_scales)
-        load_w1(1)
         load_page(0)
-        place_list = load_list("place_list", offs3)
+        load_w1(1)
         load_w1(2)
         load_page(1)
+        load_w1(3)
         gain_upper = keep.tile([P, PACK], F32, name="gain_upper")
         nc.sync.dma_start(out=gain_upper[:], in_=gain[H // 2 :].rearrange("(p t) -> p t", t=PACK))
         nc.sync.dma_start(out=low_rows[0:CALL_TILES, :], in_=low.rearrange("(n p) -> n p", p=P))
@@ -142,25 +140,25 @@ def tile_list_birdsong_retrieval_kernel(
             nc.vector.tensor_copy(scales[:], tab_plane[:].indirect(part_of(clip_list, BANK * half, BANK)))
             v_scales.append(scales)
         for b in range(PACK):
-            nc.vector.tensor_scalar(lower_weights[b][:], wgs_tile[:], amp_gain[:, b : b + 1], None, ALU.mult)
+            nc.gpsimd.tensor_scalar(lower_weights[b][:], wgs_tile[:], amp_gain[:, b : b + 1], 0.0, ALU.mult, ALU.add)
+        call_rows = keep.tile([P, S2], U8, name="call_rows", align_bytes=64)
+        nc.vector.tensor_copy(call_rows[:], tab2_plane[:].indirect(call_list[:]))
 
         def gather_clip_words(half):
             codes = keep.tile([P, BANK], U32, name="v_codes%d" % half, align_bytes=64)
             nc.vector.tensor_copy(codes[:], tab_tile[:].indirect(part_of(clip_list, BANK * half, BANK)))
             v_codes.append(codes)
 
-        gather_clip_words(0)
 
         w1_codes = {}
 
-        def quantise_w1(lo, hi):
-            load = min(lo // P, len(W1_LOADS) - 1)
-            first = W1_LOADS[load][0]
+        def quantise_w1(load):
+            lo, hi = W1_LOADS[load]
             grouped = keep.tile([P, (hi - lo) * PACK], BF16, name="w1_grouped%d" % lo, align_bytes=64)
             order = "p (c i j) -> p c j i" if lo < H // 2 else "p (i c j) -> p c j i"
             nc.scalar.copy(
                 out=grouped[:].rearrange(order, i=4, j=PACK),
-                in_=w1_raw[load][:, :, lo - first : hi - first].rearrange("p j (c i) -> p c j i", i=4),
+                in_=w1_raw[load][:].rearrange("p j (c i) -> p c j i", i=4),
             )
             codes = keep.tile([P, hi - lo], U32, name="w1_codes%d" % lo, align_bytes=64)
             scales = keep.tile([P, hi - lo], U8, name="w1_scales%d" % lo, align_bytes=64)
@@ -195,17 +193,16 @@ def tile_list_birdsong_retrieval_kernel(
             def fold(folded, piece):
                 half, c0 = divmod(PIECE * piece, BANK)
                 acc = banks[piece]
-                for c in range(0, PIECE, P):
-                    cols = slice(c0 + c, c0 + c + P)
-                    moving, moving_scale = v_codes[half][:, cols].bitcast(FP8X4), v_scales[half][:, cols]
-                    nc.tensor.matmul_mx(
-                        out=acc[:, c : c + P], lhsT=w4_codes.bitcast(FP4X4), lhsT_scale=w4_bytes,
-                        rhs=moving, rhs_scale=moving_scale, start=True, stop=False,
-                    )
-                    nc.tensor.matmul_mx(
-                        out=acc[:, c : c + P], lhsT=codes.bitcast(FP8X4), lhsT_scale=scales,
-                        rhs=moving, rhs_scale=moving_scale, start=False, stop=True,
-                    )
+                cols = slice(c0, c0 + PIECE)
+                moving, moving_scale = v_codes[half][:, cols].bitcast(FP8X4), v_scales[half][:, cols]
+                nc.tensor.matmul_mx(
+                    out=acc[:, 0:PIECE], lhsT=w4_codes.bitcast(FP4X4), lhsT_scale=w4_bytes,
+                    rhs=moving, rhs_scale=moving_scale, start=True, stop=False,
+                )
+                nc.tensor.matmul_mx(
+                    out=acc[:, 0:PIECE], lhsT=codes.bitcast(FP8X4), lhsT_scale=scales,
+                    rhs=moving, rhs_scale=moving_scale, start=False, stop=True,
+                )
                 nc.scalar.activation(out=folded, in_=acc[:, 0:PIECE], func=ACT.Abs, bias=-math.pi / 4)
 
             def cosine(unit, folded):
@@ -215,11 +212,14 @@ def tile_list_birdsong_retrieval_kernel(
                 nc.scalar.activation(out=result, in_=unit, func=ACT.Copy, scale=amp_gain[:, b : b + 1])
 
             if b == 0:
-                folded = ring.tile([P, S], F32, name="folded", tag="work", bufs=3)
                 for first, width in FIRST_PIECES:
-                    for c in range(first, first + width, PIECE):
-                        fold(folded[:, c : c + PIECE], c // PIECE)
-                    cosine(wave[:, first : first + width], folded[:, first : first + width])
+                    if first + width < S:
+                        folded = ring.tile([P, width], F32, name="folded", tag="work", bufs=3)
+                    else:
+                        folded = stage.tile([P, width], F32, name="folded0", offset=4 * PACK * W1_LOADS[1][0])
+                    for c in range(0, width, PIECE):
+                        fold(folded[:, c : c + PIECE], (first + c) // PIECE)
+                    cosine(wave[:, first : first + width], folded[:])
             elif b == LAST:
                 for half in range(S // BANK):
                     folded = ring.tile([P, BANK], F32, name="folded_half", tag="pairs%d" % (2 * half), align_bytes=64)
@@ -229,7 +229,10 @@ def tile_list_birdsong_retrieval_kernel(
                     cosine(unit[:], folded[:])
                     amplify(wave[:, BANK * half : BANK * (half + 1)], unit[:])
             else:
-                folded = ring.tile([P, S], F32, name="folded", tag="work", bufs=3)
+                if b + 1 < len(W1_LOADS):
+                    folded = stage.tile([P, S], F32, name="folded%d" % b, offset=4 * PACK * W1_LOADS[b + 1][0])
+                else:
+                    folded = ring.tile([P, S], F32, name="folded", tag="work", bufs=3)
                 for c in range(0, S, PIECE):
                     fold(folded[:, c : c + PIECE], c // PIECE)
                 if b < PACK:
@@ -293,9 +296,8 @@ def tile_list_birdsong_retrieval_kernel(
                 in_=pages[b][:, BANK * q : BANK * (q + 1)],
             )
 
-        def weave(q):
+        def weave(q, copy):
             tile = keep.tile([P, 2 * BANK], F32, name="woven1", tag="turned%d" % q, align_bytes=64)
-            copy = nc.scalar.copy if q < CHUNKS - 1 else nc.vector.tensor_copy
             copy(
                 out=tile[:].rearrange("p (c u) -> p c u", u=2),
                 in_=pairs[q][:].bitcast(F32).rearrange("p (u c) -> p c u", u=2),
@@ -309,21 +311,25 @@ def tile_list_birdsong_retrieval_kernel(
             nc.vector.quantize_mx(out=codes[:].bitcast(FP8X4), scales=scales, in_=woven[a, q][:].bitcast(BF16))
             page_codes[a, q] = (codes, scales)
 
-        quantise_w1(*W1_GROUPS[0])
+        quantise_w1(0)
+        gather_clip_words(0)
         gather_clip_words(1)
+        order_upper_w4()
         wgs_upper = slab.tile([P, PACK * S], F32, name="wgs_upper", align_bytes=64, offset=0)
         for quad in (0, 2, 1, 3):
             nc.sync.dma_start(out=wgs_upper[32 * quad : 32 * (quad + 1), :], in_=wgs.rearrange("(m t) j -> m (t j)", t=PACK))
-        load_scale_rows(nc.sync, tab2_plane, tab2_scales)
-        call_list = load_list("call_list", offs2)
         read_list = load_list("read_list", offs4)
+        for a in range(PASSES):
+            for r in range(4):
+                nc.sync.dma_start(
+                    out=call_scales[4 * a + r : P : 32, :].bitcast(I32),
+                    in_=call_rows[64 * a + 4 * r : 64 * (a + 1) : 16, :].bitcast(I32),
+                )
 
-        quantise_w1(*W1_GROUPS[1])
         for b in range(AHEAD):
+            quantise_w1(b + 1)
             phases(b)
-        for group in W1_GROUPS[AHEAD:]:
-            quantise_w1(*group)
-        order_upper_w4()
+        quantise_w1(AHEAD + 1)
         nc.vector.tensor_scalar(amp_gain[:, PACK:], gain_upper[:], half_amp[:], 2.0, ALU.mult, ALU.mult)
         nc.tensor.transpose(banks[6][:, 0:P], low_rows[:], ident[:])
         floor = keep.tile([P, CALL_TILES], F32, name="floor")
@@ -350,11 +356,7 @@ def tile_list_birdsong_retrieval_kernel(
                     round_page(b, q)
 
         half_calls = S2 // 2
-        call_codes, call_scales = [], []
-
-        def gather_call_scales(tile, half):
-            nc.vector.tensor_copy(tile[:], tab2_plane[:].indirect(part_of(call_list, half_calls * half, half_calls)))
-            call_scales.append(tile)
+        call_codes = []
 
         def gather_call_words(tile, half, a):
             nc.vector.tensor_copy(
@@ -362,20 +364,31 @@ def tile_list_birdsong_retrieval_kernel(
                 tab2_tiles[a][:].indirect(part_of(call_list, half_calls * half, half_calls)),
             )
 
-        late_scales = slab.tile([P, T2], U8, name="late_scales", align_bytes=64, offset=4096)
-        gather_call_scales(slab.tile([P, half_calls], U8, name="call_scales0", align_bytes=64, offset=8192), 0)
-        call_codes.append(slab.tile([P, PASSES * half_calls], U32, name="call_codes0", align_bytes=64, offset=0))
-        gather_call_words(call_codes[0], 0, 0)
-        for q in range(CHUNKS):
+        def quantise_lower(q):
             quantise_page(0, q, late_scales[:, BANK * q : BANK * (q + 1)])
-        gather_call_words(call_codes[0], 0, 1)
-        for q in (0, 1, 3, 2):
-            round_page(LAST, q)
-            weave(q)
+
+        def quantise_upper(q):
             last_scales = keep.tile([P, BANK], U8, name="page_scales1_%d" % q, align_bytes=64)
             quantise_page(1, q, last_scales[:])
-        gather_call_scales(ring.tile([P, half_calls], U8, name="call_scales1", tag="pairs3", align_bytes=64), 1)
-        call_codes.append(keep.tile([P, PASSES * half_calls], U32, name="call_codes1", tag="turned2", align_bytes=64))
+
+        late_scales = slab.tile([P, T2], U8, name="late_scales", align_bytes=64, offset=4096)
+        call_codes.append(slab.tile([P, PASSES * half_calls], U32, name="call_codes0", align_bytes=64, offset=0))
+        for q in range(CHUNKS):
+            round_page(LAST, q)
+            if q >= VECTOR_WEAVES:
+                weave(q, nc.scalar.copy)
+        gather_call_words(call_codes[0], 0, 0)
+        for q in range(VECTOR_WEAVES):
+            weave(q, nc.vector.tensor_copy)
+            quantise_lower(q)
+        for q in range(VECTOR_WEAVES):
+            quantise_upper(q)
+        gather_call_words(call_codes[0], 0, 1)
+        for q in range(VECTOR_WEAVES, CHUNKS):
+            quantise_lower(q)
+        for q in range(VECTOR_WEAVES, CHUNKS):
+            quantise_upper(q)
+        call_codes.append(keep.tile([P, PASSES * half_calls], U32, name="call_codes1", tag="turned3", align_bytes=64))
         for a in range(PASSES):
             gather_call_words(call_codes[1], 1, a)
 
@@ -385,7 +398,7 @@ def tile_list_birdsong_retrieval_kernel(
             nc.tensor.matmul_mx(
                 out=banks[(CHUNKS * n + q) % 8][:],
                 lhsT=call_codes[half][:, half_calls * a + c0 : half_calls * a + c0 + P].bitcast(FP8X4),
-                lhsT_scale=call_scales[half][4 * a : P, c0 : c0 + P],
+                lhsT_scale=call_scales[4 * a : P, P * n : P * (n + 1)],
                 rhs=codes[:].bitcast(FP8X4), rhs_scale=scales, start=(a == 0), stop=(a == PASSES - 1),
             )
 
@@ -400,30 +413,29 @@ def tile_list_birdsong_retrieval_kernel(
 
         spare_tags = list(range(PASSES * CHUNKS))
 
-        def finish(n, e):
-            cuts = (0, 512, 768, 1024) if n == CALL_TILES - 1 else (0, PICKS)
-            for first, end in zip(cuts, cuts[1:]):
-                width = end - first
-                if first == 0:
-                    picked = ring.tile([P, width], F32, name="picked", tag="wave", bufs=4)
-                else:
-                    picked = ring.tile([P, width], F32, name="picked_late", tag="work", bufs=3)
-                nc.vector.tensor_copy(picked[:], e[:].indirect(part_of(read_list, first, width)))
+        def finish(piece, n, first, width, e):
+            picked = keep.tile([P, width], F32, name="picked%d" % piece)
+            nc.vector.tensor_copy(picked[:], e[:].indirect(part_of(read_list, first, width)))
+            bound = floor[:, n : n + 1]
+            if piece < SQUARE_ON_GPSIMD:
+                result = keep.tile([P, width], F32, name="result%d" % piece)
+                nc.gpsimd.tensor_scalar(picked[:], picked[:], FLOAT_MAX, bound, ALU.min, ALU.max)
+                nc.gpsimd.tensor_tensor(result[:], picked[:], picked[:], ALU.mult)
+            elif piece < len(pieces) - 1:
                 result = keep.tile([P, width], F32, name="result", tag="codes%d" % spare_tags.pop(), align_bytes=64)
-                if first > 0:
-                    nc.vector.tensor_scalar(picked[:], picked[:], floor[:, n : n + 1], None, ALU.max)
-                    nc.vector.tensor_tensor(result[:], picked[:], picked[:], ALU.mult)
-                else:
-                    nc.gpsimd.tensor_scalar(picked[:], picked[:], FLOAT_MAX, floor[:, n : n + 1], ALU.min, ALU.max)
-                    if n < SQUARE_ON_GPSIMD:
-                        nc.gpsimd.tensor_tensor(result[:], picked[:], picked[:], ALU.mult)
-                    else:
-                        nc.scalar.activation(out=result[:], in_=picked[:], func=ACT.Square)
-                nc.sync.dma_start(out=out[P * n : P * (n + 1), first : first + width], in_=result[:])
+                nc.gpsimd.tensor_scalar(picked[:], picked[:], FLOAT_MAX, bound, ALU.min, ALU.max)
+                nc.scalar.activation(out=result[:], in_=picked[:], func=ACT.Square)
+            else:
+                result = keep.tile([P, width], F32, name="result%d" % piece)
+                nc.vector.tensor_scalar(picked[:], picked[:], bound, None, ALU.max)
+                nc.vector.tensor_tensor(result[:], picked[:], picked[:], ALU.mult)
+            nc.sync.dma_start(out=out[P * n : P * (n + 1), first : first + width], in_=result[:])
 
         for q in range(CHUNKS):
             for n in range(2):
                 product(n, q, 0)
         score_tiles = [scores(n) for n in range(CALL_TILES)]
-        for n in range(CALL_TILES):
-            finish(n, score_tiles[n])
+        pieces = [(n, first, BANK) for n in range(CALL_TILES) for first in range(0, PICKS, BANK)]
+        pieces = pieces[:-1] + [(CALL_TILES - 1, BANK, PIECE), (CALL_TILES - 1, BANK + PIECE, PIECE)]
+        for piece, (n, first, width) in enumerate(pieces):
+            finish(piece, n, first, width, score_tiles[n])

@@ -26,14 +26,19 @@ ROW_TILES = H // P
 PASSES = H // (P * PACK)
 CHUNKS = T2 // BANK
 CALL_TILES = S2 // P
+HALF_CALLS = S2 // 2
 LAST = ROW_TILES - 1
 W1_LOADS = ((0, 128), (128, 256), (256, 512), (512, 1024))
 AHEAD = 2
 PIECE = 256
+FIRST_PIECES = ((0, PIECE), (PIECE, PIECE), (BANK, BANK))
+LOWER_BACK = {4: (0,), 5: (1,), 6: (2, 3)}
+STAGED = {1: 4 * PACK * 256, 2: 4 * PACK * 256, 3: 4 * PACK * 512}
+FIRST_FOLD = 4 * PACK * H
+FOLDED = 5
 SQUARE_ON_GPSIMD = 2
-VECTOR_WEAVES = 1
+VECTOR_CHUNK = 3
 FLOAT_MAX = 3.4028234663852886e38
-FIRST_PIECES = ((0, 256), (256, 256), (512, 512))
 
 
 def tile_list_birdsong_retrieval_kernel(
@@ -71,12 +76,12 @@ def tile_list_birdsong_retrieval_kernel(
         nc.vector.memset(zero[:], 0.0)
         half_amp = keep.tile([P, 1], F32, name="half_amp")
         nc.scalar.activation(out=half_amp[:], in_=zero[:], func=ACT.Sin, bias=math.pi / 4)
-        tab2_plane = keep.tile([P, T3], U8, name="tab2_plane", align_bytes=64)
-        nc.vector.memset(tab2_plane[:].bitcast(I32), 0)
+        tab2_rows = keep.tile([P, T3], U8, name="tab2_rows", align_bytes=64)
+        nc.vector.memset(tab2_rows[:].bitcast(I32), 0)
 
-        vectors = keep.tile([P, P], F32, name="vectors")
-        nc.gpsimd.memset(vectors[:], 0.0)
-        nc.gpsimd.dma_start(out=vectors[0:PACK, :], in_=gain[0 : H // 2].rearrange("(b p) -> b p", p=P))
+        gain_rows = keep.tile([P, P], F32, name="gain_rows")
+        nc.gpsimd.memset(gain_rows[:], 0.0)
+        nc.gpsimd.dma_start(out=gain_rows[0:ROW_TILES, :], in_=gain.rearrange("(b p) -> b p", p=P))
         ident = keep.tile([P, P], F32, name="ident")
         make_identity(nc, ident[:])
         call_scales = keep.tile([P, S2], U8, name="call_scales", align_bytes=64)
@@ -96,68 +101,67 @@ def tile_list_birdsong_retrieval_kernel(
 
         def load_page(b):
             page = ring.tile([P, T2], F32, name="page", tag="rows", bufs=4)
-            if b < PACK:
-                rows = page0[P * b : P * (b + 1), :]
-            else:
-                rows = page0[H // 2 :, :].rearrange("(p t) c -> p t c", t=PACK)[:, b - PACK, :]
-            nc.sync.dma_start(out=page[:], in_=rows)
+            nc.sync.dma_start(out=page[:], in_=page0[P * b : P * (b + 1), :])
             pages.append(page)
 
         clip_list = load_list("clip_list", offs)
         call_list = load_list("call_list", offs2)
-        wgs_tile = shelf.tile([P, S], F32, name="wgs_tile", align_bytes=64, offset=(PACK - 1) * 4 * S)
+        wgs_tile = shelf.tile([P, S], F32, name="wgs_tile", align_bytes=64, offset=FOLDED * 4 * S)
         nc.sync.dma_start(out=wgs_tile[:], in_=wgs)
         load_w1(0)
         load_plane(tab_plane, tab_scales)
-        nc.sync.dma_start(out=tab2_plane[0:P:4, :].bitcast(I32), in_=tab2_scales.rearrange("a q t -> (a q) t").bitcast(I32))
+        nc.sync.dma_start(out=tab2_rows[0:P:4, :].bitcast(I32), in_=tab2_scales.rearrange("a q t -> (a q) t").bitcast(I32))
         tab_tile = slab.tile([P, T], U32, name="tab_tile", align_bytes=64, offset=0)
         nc.sync.dma_start(out=tab_tile[:].bitcast(I32), in_=tab_words[0].rearrange("p t i -> p (t i)").bitcast(I32))
         place_list = load_list("place_list", offs3)
         w4_tile = keep.tile([P, 2 * H], U8, name="w4_tile", align_bytes=64)
         nc.sync.dma_start(out=w4_tile[:].bitcast(I32), in_=w4_words[0].bitcast(I32))
         load_plane(w4_plane, w4_scales)
-        load_page(0)
         load_w1(1)
+        load_page(0)
         load_w1(2)
         load_page(1)
         load_w1(3)
-        gain_upper = keep.tile([P, PACK], F32, name="gain_upper")
-        nc.sync.dma_start(out=gain_upper[:], in_=gain[H // 2 :].rearrange("(p t) -> p t", t=PACK))
         nc.sync.dma_start(out=low_rows[0:CALL_TILES, :], in_=low.rearrange("(n p) -> n p", p=P))
         load_page(2)
         load_page(3)
-        banks = [psum.tile([P, BANK], F32, name="bank%d" % i) for i in range(8)]
-        columns = banks[7]
-        nc.tensor.transpose(columns[:, 0:P], vectors[:], ident[:])
-        amp_gain = keep.tile([P, ROW_TILES], F32, name="amp_gain")
-        nc.vector.tensor_scalar(amp_gain[:, 0:PACK], columns[:, 0:PACK], half_amp[:], 2.0, ALU.mult, ALU.mult)
+        read_list = load_list("read_list", offs4)
 
-        lower_weights = [shelf.tile([P, S], F32, name="weights%d" % b, align_bytes=64, offset=4 * S * b) for b in range(PACK - 1)] + [wgs_tile]
+        banks = [psum.tile([P, BANK], F32, name="bank%d" % i) for i in range(8)]
+        nc.tensor.transpose(banks[7][:, 0:P], gain_rows[:], ident[:])
+        amp_gain = keep.tile([P, ROW_TILES], F32, name="amp_gain")
+        nc.vector.tensor_scalar(amp_gain[:], banks[7][:, 0:ROW_TILES], half_amp[:], 2.0, ALU.mult, ALU.mult)
+        weights = []
+        for b in range(FOLDED):
+            folded_weights = shelf.tile([P, S], F32, name="weights%d" % b, align_bytes=64, offset=4 * S * b)
+            nc.gpsimd.tensor_scalar(folded_weights[:], wgs_tile[:], amp_gain[:, b : b + 1], 0.0, ALU.mult, ALU.add)
+            weights.append(folded_weights)
 
         v_codes, v_scales = [], []
         for half in range(S // BANK):
             scales = keep.tile([P, BANK], U8, name="v_scales%d" % half, align_bytes=64)
             nc.vector.tensor_copy(scales[:], tab_plane[:].indirect(part_of(clip_list, BANK * half, BANK)))
             v_scales.append(scales)
-        for b in range(PACK):
-            nc.gpsimd.tensor_scalar(lower_weights[b][:], wgs_tile[:], amp_gain[:, b : b + 1], 0.0, ALU.mult, ALU.add)
         call_rows = keep.tile([P, S2], U8, name="call_rows", align_bytes=64)
-        nc.vector.tensor_copy(call_rows[:], tab2_plane[:].indirect(call_list[:]))
-
-        def gather_clip_words(half):
-            codes = keep.tile([P, BANK], U32, name="v_codes%d" % half, align_bytes=64)
-            nc.vector.tensor_copy(codes[:], tab_tile[:].indirect(part_of(clip_list, BANK * half, BANK)))
-            v_codes.append(codes)
-
+        nc.vector.tensor_copy(call_rows[:], tab2_rows[:].indirect(call_list[:]))
+        for a in range(PASSES):
+            for r in range(4):
+                nc.sync.dma_start(
+                    out=call_scales[4 * a + r : P : 32, :].bitcast(I32),
+                    in_=call_rows[64 * a + 4 * r : 64 * (a + 1) : 16, :].bitcast(I32),
+                )
 
         w1_codes = {}
 
         def quantise_w1(load):
             lo, hi = W1_LOADS[load]
-            grouped = keep.tile([P, (hi - lo) * PACK], BF16, name="w1_grouped%d" % lo, align_bytes=64)
-            order = "p (c i j) -> p c j i" if lo < H // 2 else "p (i c j) -> p c j i"
+            if load < 2:
+                grouped = keep.tile([P, (hi - lo) * PACK], BF16, name="w1_grouped%d" % lo, align_bytes=64)
+            else:
+                place = FIRST_FOLD if load == 2 else STAGED[2]
+                grouped = stage.tile([P, (hi - lo) * PACK], BF16, name="w1_grouped%d" % lo, align_bytes=64, offset=place)
             nc.scalar.copy(
-                out=grouped[:].rearrange(order, i=4, j=PACK),
+                out=grouped[:].rearrange("p (c i j) -> p c j i", i=4, j=PACK),
                 in_=w1_raw[load][:].rearrange("p j (c i) -> p c j i", i=4),
             )
             codes = keep.tile([P, hi - lo], U32, name="w1_codes%d" % lo, align_bytes=64)
@@ -166,246 +170,171 @@ def tile_list_birdsong_retrieval_kernel(
             for c0 in range(lo, hi, P):
                 w1_codes[c0 // P] = (codes[:, c0 - lo : c0 - lo + P], scales[:, c0 - lo : c0 - lo + P])
 
-        w4_upper = keep.tile([P, H], U8, name="w4_upper", align_bytes=64)
-        w4_upper_plane = keep.tile([P, H // 2], U8, name="w4_upper_plane", align_bytes=64)
+        quantise_w1(0)
+        for half in range(S // BANK):
+            codes = keep.tile([P, BANK], U32, name="v_codes%d" % half, align_bytes=64)
+            nc.vector.tensor_copy(codes[:], tab_tile[:].indirect(part_of(clip_list, BANK * half, BANK)))
+            v_codes.append(codes)
 
-        def order_upper_w4():
-            nc.vector.tensor_copy(
-                out=w4_upper[:].bitcast(U16).rearrange("p (t m) -> p m t", t=PACK),
-                in_=w4_tile[:, H:].bitcast(U16).rearrange("p (m t) -> p m t", t=PACK),
-            )
-            nc.vector.tensor_copy(
-                out=w4_upper_plane[:].rearrange("p (t m) -> p m t", t=PACK),
-                in_=w4_plane[:, H // 2 :].rearrange("p (m t) -> p m t", t=PACK),
-            )
+        waves = {}
 
-        factors = {}
+        def fold(b, folded, first, width, acc):
+            half, c0 = divmod(first, BANK)
+            moving, moving_scale = v_codes[half][:, c0 : c0 + width].bitcast(FP8X4), v_scales[half][:, c0 : c0 + width]
+            codes, scales = w1_codes[b]
+            nc.tensor.matmul_mx(
+                out=acc[:, 0:width], lhsT=w4_tile[:, 2 * P * b : 2 * P * (b + 1)].bitcast(FP4X4),
+                lhsT_scale=w4_plane[:, P * b : P * (b + 1)], rhs=moving, rhs_scale=moving_scale, start=True, stop=False,
+            )
+            nc.tensor.matmul_mx(
+                out=acc[:, 0:width], lhsT=codes.bitcast(FP8X4), lhsT_scale=scales,
+                rhs=moving, rhs_scale=moving_scale, start=False, stop=True,
+            )
+            nc.scalar.activation(out=folded, in_=acc[:, 0:width], func=ACT.Abs, bias=-math.pi / 4)
+
+        def cosine(unit, folded):
+            nc.scalar.activation(out=unit, in_=folded, func=ACT.Sin, scale=-1.0, bias=math.pi / 2)
 
         def phases(b):
             wave = ring.tile([P, S], F32, name="wave", tag="wave", bufs=4)
-            codes, scales = w1_codes[b]
-            if b < PACK:
-                w4_codes, w4_bytes = w4_tile[:, 2 * P * b : 2 * P * (b + 1)], w4_plane[:, P * b : P * (b + 1)]
-            else:
-                t = b - PACK
-                w4_codes, w4_bytes = w4_upper[:, 2 * P * t : 2 * P * (t + 1)], w4_upper_plane[:, P * t : P * (t + 1)]
-
-            def fold(folded, piece):
-                half, c0 = divmod(PIECE * piece, BANK)
-                acc = banks[piece]
-                cols = slice(c0, c0 + PIECE)
-                moving, moving_scale = v_codes[half][:, cols].bitcast(FP8X4), v_scales[half][:, cols]
-                nc.tensor.matmul_mx(
-                    out=acc[:, 0:PIECE], lhsT=w4_codes.bitcast(FP4X4), lhsT_scale=w4_bytes,
-                    rhs=moving, rhs_scale=moving_scale, start=True, stop=False,
-                )
-                nc.tensor.matmul_mx(
-                    out=acc[:, 0:PIECE], lhsT=codes.bitcast(FP8X4), lhsT_scale=scales,
-                    rhs=moving, rhs_scale=moving_scale, start=False, stop=True,
-                )
-                nc.scalar.activation(out=folded, in_=acc[:, 0:PIECE], func=ACT.Abs, bias=-math.pi / 4)
-
-            def cosine(unit, folded):
-                nc.scalar.activation(out=unit, in_=folded, func=ACT.Sin, scale=-1.0, bias=math.pi / 2)
-
-            def amplify(result, unit):
-                nc.scalar.activation(out=result, in_=unit, func=ACT.Copy, scale=amp_gain[:, b : b + 1])
-
             if b == 0:
-                for first, width in FIRST_PIECES:
-                    if first + width < S:
-                        folded = ring.tile([P, width], F32, name="folded", tag="work", bufs=3)
+                for piece, (first, width) in enumerate(FIRST_PIECES):
+                    if width < BANK:
+                        folded = ring.tile([P, width], F32, name="folded", tag="work", bufs=2)
                     else:
-                        folded = stage.tile([P, width], F32, name="folded0", offset=4 * PACK * W1_LOADS[1][0])
-                    for c in range(0, width, PIECE):
-                        fold(folded[:, c : c + PIECE], (first + c) // PIECE)
+                        folded = stage.tile([P, width], F32, name="folded0", align_bytes=64, offset=FIRST_FOLD)
+                    fold(b, folded[:], first, width, banks[4 + piece])
                     cosine(wave[:, first : first + width], folded[:])
-            elif b == LAST:
-                for half in range(S // BANK):
-                    folded = ring.tile([P, BANK], F32, name="folded_half", tag="pairs%d" % (2 * half), align_bytes=64)
-                    unit = ring.tile([P, BANK], F32, name="unit_half", tag="pairs%d" % (2 * half + 1), align_bytes=64)
-                    for c in range(0, BANK, PIECE):
-                        fold(folded[:, c : c + PIECE], (BANK * half + c) // PIECE)
-                    cosine(unit[:], folded[:])
-                    amplify(wave[:, BANK * half : BANK * (half + 1)], unit[:])
             else:
-                if b + 1 < len(W1_LOADS):
-                    folded = stage.tile([P, S], F32, name="folded%d" % b, offset=4 * PACK * W1_LOADS[b + 1][0])
-                else:
-                    folded = ring.tile([P, S], F32, name="folded", tag="work", bufs=3)
-                for c in range(0, S, PIECE):
-                    fold(folded[:, c : c + PIECE], c // PIECE)
-                if b < PACK:
+                folded = stage.tile([P, S], F32, name="folded%d" % b, offset=STAGED[min(b, 3)])
+                width = PIECE if b >= AHEAD else BANK
+                for c in range(0, S, width):
+                    fold(b, folded[:, c : c + width], c, width, banks[c // width])
+                if b < FOLDED:
                     cosine(wave[:], folded[:])
                 else:
-                    unit = ring.tile([P, S], F32, name="unit", tag="work", bufs=3)
-                    cosine(unit[:], folded[:])
-                    amplify(wave[:], unit[:])
-            factors[b] = wave
+                    cosine(folded[:], folded[:])
+                    nc.scalar.activation(out=wave[:], in_=folded[:], func=ACT.Copy, scale=amp_gain[:, b : b + 1])
+            waves[b] = wave
 
         def scatter(b):
-            wave = factors[b]
-            if b < PACK:
-                weights = lower_weights[b][:]
-            else:
-                weights = wgs_upper[:, S * (b - PACK) : S * (b - PACK + 1)]
+            wave = waves[b]
+            factor = weights[b] if b < FOLDED else wgs_tile
             for first, width in FIRST_PIECES if b == 0 else ((0, S),):
                 cols = slice(first, first + width)
                 nc.vector.tensor_tensor(
-                    pages[b][:].indirect(part_of(place_list, first, width)), wave[:, cols], weights[:, cols], ALU.mult
+                    pages[b][:].indirect(part_of(place_list, first, width)), wave[:, cols], factor[:, cols], ALU.mult
                 )
 
         turned = {}
 
         def turn_page(b, q):
+            a, quad = divmod(b, PACK)
             if b == 0:
-                turned[q] = keep.tile([P, 4 * P * PACK], BF16, name="turned", tag="turned%d" % q, align_bytes=64)
+                turned[a, q] = keep.tile([P, PACK * BANK], BF16, name="turned0", tag="turned%d" % q, align_bytes=64)
+            elif b == PACK:
+                turned[a, q] = slab.tile([P, PACK * BANK], BF16, name="turned1_%d" % q, align_bytes=64, offset=2 * PACK * BANK * q)
             bank = banks[q]
             for i in range(4):
                 c0 = BANK * q + P * i
                 nc.tensor.transpose(bank[:, P * i : P * (i + 1)], pages[b][:, c0 : c0 + P], ident[:])
             nc.scalar.copy(
-                out=turned[q][:].rearrange("c (i u p e) -> c i u p e", i=4, u=2, e=2)[:, :, :, 32 * b : 32 * (b + 1), :],
+                out=turned[a, q][:].rearrange("c (i u p e) -> c i u p e", i=4, u=2, e=2)[:, :, :, 32 * quad : 32 * (quad + 1), :],
                 in_=bank[:].rearrange("c (i p u e) -> c i u p e", i=4, u=2, e=2),
             )
 
         woven = {}
 
-        def turn_back(q):
-            tile = keep.tile([P, 2 * BANK], F32, name="woven0_%d" % q, align_bytes=64)
-            words = turned[q][:].bitcast(F32)
+        def turn_back(a, q, first_bank, copy):
+            if a == 0:
+                tile = keep.tile([P, 2 * BANK], F32, name="woven0_%d" % q, align_bytes=64)
+            else:
+                tile = keep.tile([P, 2 * BANK], F32, name="woven1", tag="turned%d" % q, align_bytes=64)
+            words = turned[a, q][:].bitcast(F32)
             for k in range(2):
-                bank = banks[4 + (2 * q + k) % 4]
+                bank = banks[first_bank + k]
                 for j in range(4):
                     c0 = BANK * k + P * j
                     nc.tensor.transpose(bank[:, P * j : P * (j + 1)], words[:, c0 : c0 + P], ident[:])
-                nc.scalar.copy(
+                copy(
                     out=tile[:, BANK * k : BANK * (k + 1)].rearrange("p (i c u) -> p i c u", i=2, u=2),
                     in_=bank[:].rearrange("p (i u c) -> p i c u", i=2, u=2),
                 )
-            woven[0, q] = tile
-
-        pairs = {}
-
-        def round_page(b, q):
-            u, e = divmod(b - PACK, 2)
-            if b == PACK:
-                pairs[q] = ring.tile([P, PACK * BANK], BF16, name="pairs", tag="pairs%d" % q, align_bytes=64)
-            nc.scalar.copy(
-                out=pairs[q][:].rearrange("p (u c e) -> p u c e", u=2, e=2)[:, u, :, e],
-                in_=pages[b][:, BANK * q : BANK * (q + 1)],
-            )
-
-        def weave(q, copy):
-            tile = keep.tile([P, 2 * BANK], F32, name="woven1", tag="turned%d" % q, align_bytes=64)
-            copy(
-                out=tile[:].rearrange("p (c u) -> p c u", u=2),
-                in_=pairs[q][:].bitcast(F32).rearrange("p (u c) -> p c u", u=2),
-            )
-            woven[1, q] = tile
-
-        page_codes = {}
-
-        def quantise_page(a, q, scales):
-            codes = keep.tile([P, BANK], U32, name="page_codes", tag="codes%d" % (PASSES * q + a), align_bytes=64)
-            nc.vector.quantize_mx(out=codes[:].bitcast(FP8X4), scales=scales, in_=woven[a, q][:].bitcast(BF16))
-            page_codes[a, q] = (codes, scales)
-
-        quantise_w1(0)
-        gather_clip_words(0)
-        gather_clip_words(1)
-        order_upper_w4()
-        wgs_upper = slab.tile([P, PACK * S], F32, name="wgs_upper", align_bytes=64, offset=0)
-        for quad in (0, 2, 1, 3):
-            nc.sync.dma_start(out=wgs_upper[32 * quad : 32 * (quad + 1), :], in_=wgs.rearrange("(m t) j -> m (t j)", t=PACK))
-        read_list = load_list("read_list", offs4)
-        for a in range(PASSES):
-            for r in range(4):
-                nc.sync.dma_start(
-                    out=call_scales[4 * a + r : P : 32, :].bitcast(I32),
-                    in_=call_rows[64 * a + 4 * r : 64 * (a + 1) : 16, :].bitcast(I32),
-                )
+            woven[a, q] = tile
 
         for b in range(AHEAD):
             quantise_w1(b + 1)
             phases(b)
-        quantise_w1(AHEAD + 1)
-        nc.vector.tensor_scalar(amp_gain[:, PACK:], gain_upper[:], half_amp[:], 2.0, ALU.mult, ALU.mult)
-        nc.tensor.transpose(banks[6][:, 0:P], low_rows[:], ident[:])
         floor = keep.tile([P, CALL_TILES], F32, name="floor")
-        nc.scalar.copy(out=floor[:], in_=banks[6][:, 0:CALL_TILES])
-        for b in range(PACK):
-            phases(b + AHEAD)
+        tab2_tiles = []
+        for b in range(ROW_TILES):
+            if b + AHEAD < ROW_TILES:
+                phases(b + AHEAD)
+            if b == 0:
+                quantise_w1(len(W1_LOADS) - 1)
             scatter(b)
+            for q in LOWER_BACK.get(b, ()):
+                turn_back(0, q, 4 + 2 * (q % 2), nc.scalar.copy)
             for q in range(CHUNKS):
                 turn_page(b, q)
-            load_page(b + PACK)
-        tab2_tiles = []
-        for a in range(PASSES):
-            words = shelf.tile([P, T3], U32, name="tab2_tile%d" % a, align_bytes=64, offset=4 * T3 * a)
-            nc.sync.dma_start(out=words[:].bitcast(I32), in_=tab2_words[a].rearrange("p t i -> p (t i)").bitcast(I32))
-            tab2_tiles.append(words)
-        for b in range(PACK + AHEAD, ROW_TILES):
-            phases(b)
-        for q in range(CHUNKS):
-            turn_back(q)
-        for b in range(PACK, ROW_TILES):
-            scatter(b)
-            if b < LAST:
-                for q in range(CHUNKS):
-                    round_page(b, q)
+            if b == 1:
+                nc.tensor.transpose(banks[0][:, 0:P], low_rows[:], ident[:])
+                nc.scalar.copy(out=floor[:], in_=banks[0][:, 0:CALL_TILES])
+            if b < PACK:
+                load_page(b + PACK)
+            if b == PACK - 1:
+                for a in range(PASSES):
+                    words = shelf.tile([P, T3], U32, name="tab2_tile%d" % a, align_bytes=64, offset=4 * T3 * a)
+                    nc.sync.dma_start(out=words[:].bitcast(I32), in_=tab2_words[a].rearrange("p t i -> p (t i)").bitcast(I32))
+                    tab2_tiles.append(words)
 
-        half_calls = S2 // 2
         call_codes = []
+        page_codes = {}
 
-        def gather_call_words(tile, half, a):
+        def gather_call_words(half, a):
             nc.vector.tensor_copy(
-                tile[:, half_calls * a : half_calls * (a + 1)],
-                tab2_tiles[a][:].indirect(part_of(call_list, half_calls * half, half_calls)),
+                call_codes[half][:, HALF_CALLS * a : HALF_CALLS * (a + 1)],
+                tab2_tiles[a][:].indirect(part_of(call_list, HALF_CALLS * half, HALF_CALLS)),
             )
 
-        def quantise_lower(q):
-            quantise_page(0, q, late_scales[:, BANK * q : BANK * (q + 1)])
+        def quantise_page(a, q):
+            if a == 0:
+                scales = late_scales[:, BANK * q : BANK * (q + 1)]
+            else:
+                scales = keep.tile([P, BANK], U8, name="page_scales1_%d" % q, align_bytes=64)[:]
+            codes = keep.tile([P, BANK], U32, name="page_codes", tag="codes%d" % (PASSES * q + a), align_bytes=64)
+            nc.vector.quantize_mx(out=codes[:].bitcast(FP8X4), scales=scales, in_=woven[a, q][:].bitcast(BF16))
+            page_codes[a, q] = (codes, scales)
 
-        def quantise_upper(q):
-            last_scales = keep.tile([P, BANK], U8, name="page_scales1_%d" % q, align_bytes=64)
-            quantise_page(1, q, last_scales[:])
-
-        late_scales = slab.tile([P, T2], U8, name="late_scales", align_bytes=64, offset=4096)
-        call_codes.append(slab.tile([P, PASSES * half_calls], U32, name="call_codes0", align_bytes=64, offset=0))
+        call_codes.append(shelf.tile([P, S2], U32, name="call_codes0", align_bytes=64, offset=FOLDED * 4 * S))
+        late_scales = shelf.tile([P, T2], U8, name="late_scales", align_bytes=64, offset=FOLDED * 4 * S + 4 * S2)
+        gather_call_words(0, 0)
         for q in range(CHUNKS):
-            round_page(LAST, q)
-            if q >= VECTOR_WEAVES:
-                weave(q, nc.scalar.copy)
-        gather_call_words(call_codes[0], 0, 0)
-        for q in range(VECTOR_WEAVES):
-            weave(q, nc.vector.tensor_copy)
-            quantise_lower(q)
-        for q in range(VECTOR_WEAVES):
-            quantise_upper(q)
-        gather_call_words(call_codes[0], 0, 1)
-        for q in range(VECTOR_WEAVES, CHUNKS):
-            quantise_lower(q)
-        for q in range(VECTOR_WEAVES, CHUNKS):
-            quantise_upper(q)
-        call_codes.append(keep.tile([P, PASSES * half_calls], U32, name="call_codes1", tag="turned3", align_bytes=64))
+            quantise_page(0, q)
+        gather_call_words(0, 1)
+        order = (0, VECTOR_CHUNK, 1, 2)
+        for place, q in enumerate(order):
+            turn_back(1, q, 4 + 2 * (place % 2), nc.vector.tensor_copy if q == VECTOR_CHUNK else nc.scalar.copy)
+        for q in order:
+            quantise_page(1, q)
+        call_codes.append(keep.tile([P, S2], U32, name="call_codes1", tag="turned%d" % order[-1], align_bytes=64))
         for a in range(PASSES):
-            gather_call_words(call_codes[1], 1, a)
+            gather_call_words(1, a)
 
         def product(n, q, a):
             codes, scales = page_codes[a, q]
             half, c0 = n // 2, P * (n % 2)
             nc.tensor.matmul_mx(
                 out=banks[(CHUNKS * n + q) % 8][:],
-                lhsT=call_codes[half][:, half_calls * a + c0 : half_calls * a + c0 + P].bitcast(FP8X4),
+                lhsT=call_codes[half][:, HALF_CALLS * a + c0 : HALF_CALLS * a + c0 + P].bitcast(FP8X4),
                 lhsT_scale=call_scales[4 * a : P, P * n : P * (n + 1)],
                 rhs=codes[:].bitcast(FP8X4), rhs_scale=scales, start=(a == 0), stop=(a == PASSES - 1),
             )
 
         def scores(n):
             e = ring.tile([P, T2], F32, name="e", tag="rows", bufs=4)
-            for q in range(CHUNKS):
-                if n >= 2:
+            for q in order:
+                if n > 0:
                     product(n, q, 0)
                 product(n, q, 1)
                 nc.scalar.copy(out=e[:, BANK * q : BANK * (q + 1)], in_=banks[(CHUNKS * n + q) % 8][:])
@@ -432,8 +361,7 @@ def tile_list_birdsong_retrieval_kernel(
             nc.sync.dma_start(out=out[P * n : P * (n + 1), first : first + width], in_=result[:])
 
         for q in range(CHUNKS):
-            for n in range(2):
-                product(n, q, 0)
+            product(0, q, 0)
         score_tiles = [scores(n) for n in range(CALL_TILES)]
         pieces = [(n, first, BANK) for n in range(CALL_TILES) for first in range(0, PICKS, BANK)]
         pieces = pieces[:-1] + [(CALL_TILES - 1, BANK, PIECE), (CALL_TILES - 1, BANK + PIECE, PIECE)]

@@ -113,12 +113,12 @@ def tile_list_birdsong_retrieval_kernel(
         nc.sync.dma_start(out=tab2_rows[0:P:4, :].bitcast(I32), in_=tab2_scales.rearrange("a q t -> (a q) t").bitcast(I32))
         tab_tile = slab.tile([P, T], U32, name="tab_tile", align_bytes=64, offset=0)
         nc.sync.dma_start(out=tab_tile[:].bitcast(I32), in_=tab_words[0].rearrange("p t i -> p (t i)").bitcast(I32))
-        place_list = load_list("place_list", offs3)
         w4_tile = keep.tile([P, 2 * H], U8, name="w4_tile", align_bytes=64)
         nc.sync.dma_start(out=w4_tile[:].bitcast(I32), in_=w4_words[0].bitcast(I32))
         load_plane(w4_plane, w4_scales)
         load_w1(1)
         load_page(0)
+        place_list = load_list("place_list", offs3)
         load_w1(2)
         load_page(1)
         load_w1(3)
@@ -244,12 +244,13 @@ def tile_list_birdsong_retrieval_kernel(
             )
 
         woven = {}
+        lower_woven = [keep.tile([P, 4 * BANK], F32, name="woven0_%d" % i, align_bytes=64) for i in range(CHUNKS // 2)]
 
         def turn_back(a, q, first_bank, copy):
             if a == 0:
-                tile = keep.tile([P, 2 * BANK], F32, name="woven0_%d" % q, align_bytes=64)
+                tile = lower_woven[q // 2][:, 2 * BANK * (q % 2) : 2 * BANK * (q % 2 + 1)]
             else:
-                tile = keep.tile([P, 2 * BANK], F32, name="woven1", tag="turned%d" % q, align_bytes=64)
+                tile = keep.tile([P, 2 * BANK], F32, name="woven1", tag="turned%d" % q, align_bytes=64)[:]
             words = turned[a, q][:].bitcast(F32)
             for k in range(2):
                 bank = banks[first_bank + k]
@@ -297,26 +298,30 @@ def tile_list_birdsong_retrieval_kernel(
                 tab2_tiles[a][:].indirect(part_of(call_list, HALF_CALLS * half, HALF_CALLS)),
             )
 
-        def quantise_page(a, q):
-            if a == 0:
-                scales = late_scales[:, BANK * q : BANK * (q + 1)]
-            else:
-                scales = keep.tile([P, BANK], U8, name="page_scales1_%d" % q, align_bytes=64)[:]
-            codes = keep.tile([P, BANK], U32, name="page_codes", tag="codes%d" % (PASSES * q + a), align_bytes=64)
-            nc.vector.quantize_mx(out=codes[:].bitcast(FP8X4), scales=scales, in_=woven[a, q][:].bitcast(BF16))
-            page_codes[a, q] = (codes, scales)
+        def quantise_lower(i):
+            scales = late_scales[:, 2 * BANK * i : 2 * BANK * (i + 1)]
+            codes = keep.tile([P, 2 * BANK], U32, name="lower_codes", tag="codes%d" % i, align_bytes=64)
+            nc.vector.quantize_mx(out=codes[:].bitcast(FP8X4), scales=scales, in_=lower_woven[i][:].bitcast(BF16))
+            for k in range(2):
+                page_codes[0, 2 * i + k] = (codes[:, BANK * k : BANK * (k + 1)], scales[:, BANK * k : BANK * (k + 1)])
+
+        def quantise_upper(q):
+            scales = keep.tile([P, BANK], U8, name="upper_scales%d" % q, align_bytes=64)
+            codes = keep.tile([P, BANK], U32, name="upper_codes", tag="codes%d" % (2 + q), align_bytes=64)
+            nc.vector.quantize_mx(out=codes[:].bitcast(FP8X4), scales=scales[:], in_=woven[1, q].bitcast(BF16))
+            page_codes[1, q] = (codes[:], scales[:])
 
         call_codes.append(shelf.tile([P, S2], U32, name="call_codes0", align_bytes=64, offset=FOLDED * 4 * S))
         late_scales = shelf.tile([P, T2], U8, name="late_scales", align_bytes=64, offset=FOLDED * 4 * S + 4 * S2)
         gather_call_words(0, 0)
-        for q in range(CHUNKS):
-            quantise_page(0, q)
+        for i in range(CHUNKS // 2):
+            quantise_lower(i)
         gather_call_words(0, 1)
         order = (0, VECTOR_CHUNK, 1, 2)
         for place, q in enumerate(order):
             turn_back(1, q, 4 + 2 * (place % 2), nc.vector.tensor_copy if q == VECTOR_CHUNK else nc.scalar.copy)
         for q in order:
-            quantise_page(1, q)
+            quantise_upper(q)
         call_codes.append(keep.tile([P, S2], U32, name="call_codes1", tag="turned%d" % order[-1], align_bytes=64))
         for a in range(PASSES):
             gather_call_words(1, a)
@@ -328,7 +333,7 @@ def tile_list_birdsong_retrieval_kernel(
                 out=banks[(CHUNKS * n + q) % 8][:],
                 lhsT=call_codes[half][:, HALF_CALLS * a + c0 : HALF_CALLS * a + c0 + P].bitcast(FP8X4),
                 lhsT_scale=call_scales[4 * a : P, P * n : P * (n + 1)],
-                rhs=codes[:].bitcast(FP8X4), rhs_scale=scales, start=(a == 0), stop=(a == PASSES - 1),
+                rhs=codes.bitcast(FP8X4), rhs_scale=scales, start=(a == 0), stop=(a == PASSES - 1),
             )
 
         def scores(n):
@@ -340,7 +345,7 @@ def tile_list_birdsong_retrieval_kernel(
                 nc.scalar.copy(out=e[:, BANK * q : BANK * (q + 1)], in_=banks[(CHUNKS * n + q) % 8][:])
             return e
 
-        spare_tags = list(range(PASSES * CHUNKS))
+        spare_tags = list(range(CHUNKS // 2 + CHUNKS))
 
         def finish(piece, n, first, width, e):
             picked = keep.tile([P, width], F32, name="picked%d" % piece)
@@ -352,7 +357,10 @@ def tile_list_birdsong_retrieval_kernel(
                 nc.gpsimd.tensor_tensor(result[:], picked[:], picked[:], ALU.mult)
             elif piece < len(pieces) - 1:
                 result = keep.tile([P, width], F32, name="result", tag="codes%d" % spare_tags.pop(), align_bytes=64)
-                nc.gpsimd.tensor_scalar(picked[:], picked[:], FLOAT_MAX, bound, ALU.min, ALU.max)
+                if width == BANK:
+                    nc.gpsimd.tensor_scalar(picked[:], picked[:], FLOAT_MAX, bound, ALU.min, ALU.max)
+                else:
+                    nc.vector.tensor_scalar(picked[:], picked[:], bound, None, ALU.max)
                 nc.scalar.activation(out=result[:], in_=picked[:], func=ACT.Square)
             else:
                 result = keep.tile([P, width], F32, name="result%d" % piece)

@@ -29,13 +29,14 @@ CALL_TILES = S2 // P
 HALF_CALLS = S2 // 2
 LAST = ROW_TILES - 1
 W1_LOADS = ((0, 128), (128, 256), (256, 512), (512, 1024))
-AHEAD = 2
+AHEAD = 3
 PIECE = 256
 FIRST_PIECES = ((0, PIECE), (PIECE, PIECE), (BANK, BANK))
 LOWER_BACK = {4: (0,), 5: (1,), 6: (2, 3)}
 STAGED = {1: 4 * PACK * 256, 2: 4 * PACK * 256, 3: 4 * PACK * 512}
 FIRST_FOLD = 4 * PACK * H
 FOLDED = 5
+PAGES = 5
 SQUARE_ON_GPSIMD = 2
 VECTOR_CHUNK = 3
 FLOAT_MAX = 3.4028234663852886e38
@@ -100,7 +101,7 @@ def tile_list_birdsong_retrieval_kernel(
         pages = []
 
         def load_page(b):
-            page = ring.tile([P, T2], F32, name="page", tag="rows", bufs=4)
+            page = ring.tile([P, T2], F32, name="page", tag="rows", bufs=PAGES)
             nc.sync.dma_start(out=page[:], in_=page0[P * b : P * (b + 1), :])
             pages.append(page)
 
@@ -125,6 +126,7 @@ def tile_list_birdsong_retrieval_kernel(
         nc.sync.dma_start(out=low_rows[0:CALL_TILES, :], in_=low.rearrange("(n p) -> n p", p=P))
         load_page(2)
         load_page(3)
+        load_page(4)
         read_list = load_list("read_list", offs4)
 
         banks = [psum.tile([P, BANK], F32, name="bank%d" % i) for i in range(8)]
@@ -196,7 +198,7 @@ def tile_list_birdsong_retrieval_kernel(
             nc.scalar.activation(out=unit, in_=folded, func=ACT.Sin, scale=-1.0, bias=math.pi / 2)
 
         def phases(b):
-            wave = ring.tile([P, S], F32, name="wave", tag="wave", bufs=4)
+            wave = ring.tile([P, S], F32, name="wave", tag="wave", bufs=AHEAD + 2)
             if b == 0:
                 for piece, (first, width) in enumerate(FIRST_PIECES):
                     if width < BANK:
@@ -207,9 +209,8 @@ def tile_list_birdsong_retrieval_kernel(
                     cosine(wave[:, first : first + width], folded[:])
             else:
                 folded = stage.tile([P, S], F32, name="folded%d" % b, offset=STAGED[min(b, 3)])
-                width = PIECE if b >= AHEAD else BANK
-                for c in range(0, S, width):
-                    fold(b, folded[:, c : c + width], c, width, banks[c // width])
+                for half in range(S // BANK):
+                    fold(b, folded[:, BANK * half : BANK * (half + 1)], BANK * half, BANK, banks[2 * (b % 2) + half])
                 if b < FOLDED:
                     cosine(wave[:], folded[:])
                 else:
@@ -234,7 +235,7 @@ def tile_list_birdsong_retrieval_kernel(
                 turned[a, q] = keep.tile([P, PACK * BANK], BF16, name="turned0", tag="turned%d" % q, align_bytes=64)
             elif b == PACK:
                 turned[a, q] = slab.tile([P, PACK * BANK], BF16, name="turned1_%d" % q, align_bytes=64, offset=2 * PACK * BANK * q)
-            bank = banks[q]
+            bank = banks[2 * ((b + AHEAD) % 2) + q % 2 if b + AHEAD < ROW_TILES else q]
             for i in range(4):
                 c0 = BANK * q + P * i
                 nc.tensor.transpose(bank[:, P * i : P * (i + 1)], pages[b][:, c0 : c0 + P], ident[:])
@@ -264,15 +265,15 @@ def tile_list_birdsong_retrieval_kernel(
             woven[a, q] = tile
 
         for b in range(AHEAD):
-            quantise_w1(b + 1)
+            if b < 2:
+                quantise_w1(b + 1)
             phases(b)
+        quantise_w1(len(W1_LOADS) - 1)
         floor = keep.tile([P, CALL_TILES], F32, name="floor")
         tab2_tiles = []
         for b in range(ROW_TILES):
             if b + AHEAD < ROW_TILES:
                 phases(b + AHEAD)
-            if b == 0:
-                quantise_w1(len(W1_LOADS) - 1)
             scatter(b)
             for q in LOWER_BACK.get(b, ()):
                 turn_back(0, q, 4 + 2 * (q % 2), nc.scalar.copy)
@@ -281,8 +282,8 @@ def tile_list_birdsong_retrieval_kernel(
             if b == 1:
                 nc.tensor.transpose(banks[0][:, 0:P], low_rows[:], ident[:])
                 nc.scalar.copy(out=floor[:], in_=banks[0][:, 0:CALL_TILES])
-            if b < PACK:
-                load_page(b + PACK)
+            if b + PAGES < ROW_TILES:
+                load_page(b + PAGES)
             if b == PACK - 1:
                 for a in range(PASSES):
                     words = shelf.tile([P, T3], U32, name="tab2_tile%d" % a, align_bytes=64, offset=4 * T3 * a)
@@ -337,7 +338,7 @@ def tile_list_birdsong_retrieval_kernel(
             )
 
         def scores(n):
-            e = ring.tile([P, T2], F32, name="e", tag="rows", bufs=4)
+            e = ring.tile([P, T2], F32, name="e", tag="rows", bufs=PAGES)
             for q in order:
                 if n > 0:
                     product(n, q, 0)

@@ -28,15 +28,17 @@ CHUNKS = T2 // BANK
 CALL_TILES = S2 // P
 HALF_CALLS = S2 // 2
 LAST = ROW_TILES - 1
-W1_LOADS = ((0, 128), (128, 256), (256, 512), (512, 1024))
+W1_LOADS = ((0, 256), (256, 512), (512, 768), (768, 1024))
 AHEAD = 3
 PIECE = 256
 FIRST_PIECES = ((0, PIECE), (PIECE, PIECE), (BANK, BANK))
 LOWER_BACK = {4: (0,), 5: (1,), 6: (2, 3)}
-STAGED = {1: 4 * PACK * 256, 2: 4 * PACK * 256, 3: 4 * PACK * 512}
+FOLDED_AT = {1: 4096, 2: 6144, 3: 12288}
+GROUPED_AT = {1: 16384, 2: 4096, 3: 6144}
 FIRST_FOLD = 4 * PACK * H
-FOLDED = 5
+FOLDED = 2
 PAGES = 5
+WGS_AT = 4 * max(FOLDED * S, PASSES * T3)
 SQUARE_ON_GPSIMD = 2
 VECTOR_CHUNK = 3
 FLOAT_MAX = 3.4028234663852886e38
@@ -107,8 +109,7 @@ def tile_list_birdsong_retrieval_kernel(
 
         clip_list = load_list("clip_list", offs)
         call_list = load_list("call_list", offs2)
-        wgs_tile = shelf.tile([P, S], F32, name="wgs_tile", align_bytes=64, offset=FOLDED * 4 * S)
-        nc.sync.dma_start(out=wgs_tile[:], in_=wgs)
+        place_list = load_list("place_list", offs3)
         load_w1(0)
         load_plane(tab_plane, tab_scales)
         nc.sync.dma_start(out=tab2_rows[0:P:4, :].bitcast(I32), in_=tab2_scales.rearrange("a q t -> (a q) t").bitcast(I32))
@@ -117,11 +118,12 @@ def tile_list_birdsong_retrieval_kernel(
         w4_tile = keep.tile([P, 2 * H], U8, name="w4_tile", align_bytes=64)
         nc.sync.dma_start(out=w4_tile[:].bitcast(I32), in_=w4_words[0].bitcast(I32))
         load_plane(w4_plane, w4_scales)
-        load_w1(1)
+        wgs_tile = shelf.tile([P, S], F32, name="wgs_tile", align_bytes=64, offset=WGS_AT)
+        nc.sync.dma_start(out=wgs_tile[:], in_=wgs)
         load_page(0)
-        place_list = load_list("place_list", offs3)
-        load_w1(2)
+        load_w1(1)
         load_page(1)
+        load_w1(2)
         load_w1(3)
         nc.sync.dma_start(out=low_rows[0:CALL_TILES, :], in_=low.rearrange("(n p) -> n p", p=P))
         load_page(2)
@@ -133,11 +135,6 @@ def tile_list_birdsong_retrieval_kernel(
         nc.tensor.transpose(banks[7][:, 0:P], gain_rows[:], ident[:])
         amp_gain = keep.tile([P, ROW_TILES], F32, name="amp_gain")
         nc.vector.tensor_scalar(amp_gain[:], banks[7][:, 0:ROW_TILES], half_amp[:], 2.0, ALU.mult, ALU.mult)
-        weights = []
-        for b in range(FOLDED):
-            folded_weights = shelf.tile([P, S], F32, name="weights%d" % b, align_bytes=64, offset=4 * S * b)
-            nc.gpsimd.tensor_scalar(folded_weights[:], wgs_tile[:], amp_gain[:, b : b + 1], 0.0, ALU.mult, ALU.add)
-            weights.append(folded_weights)
 
         v_codes, v_scales = [], []
         for half in range(S // BANK):
@@ -157,11 +154,10 @@ def tile_list_birdsong_retrieval_kernel(
 
         def quantise_w1(load):
             lo, hi = W1_LOADS[load]
-            if load < 2:
+            if load == 0:
                 grouped = keep.tile([P, (hi - lo) * PACK], BF16, name="w1_grouped%d" % lo, align_bytes=64)
             else:
-                place = FIRST_FOLD if load == 2 else STAGED[2]
-                grouped = stage.tile([P, (hi - lo) * PACK], BF16, name="w1_grouped%d" % lo, align_bytes=64, offset=place)
+                grouped = stage.tile([P, (hi - lo) * PACK], BF16, name="w1_grouped%d" % lo, align_bytes=64, offset=GROUPED_AT[load])
             nc.scalar.copy(
                 out=grouped[:].rearrange("p (c i j) -> p c j i", i=4, j=PACK),
                 in_=w1_raw[load][:].rearrange("p j (c i) -> p c j i", i=4),
@@ -177,6 +173,12 @@ def tile_list_birdsong_retrieval_kernel(
             codes = keep.tile([P, BANK], U32, name="v_codes%d" % half, align_bytes=64)
             nc.vector.tensor_copy(codes[:], tab_tile[:].indirect(part_of(clip_list, BANK * half, BANK)))
             v_codes.append(codes)
+
+        weights = []
+        for b in range(FOLDED):
+            folded_weights = shelf.tile([P, S], F32, name="weights%d" % b, align_bytes=64, offset=4 * S * b)
+            nc.vector.tensor_scalar(folded_weights[:], wgs_tile[:], amp_gain[:, b : b + 1], None, ALU.mult)
+            weights.append(folded_weights)
 
         waves = {}
 
@@ -208,7 +210,7 @@ def tile_list_birdsong_retrieval_kernel(
                     fold(b, folded[:], first, width, banks[4 + piece])
                     cosine(wave[:, first : first + width], folded[:])
             else:
-                folded = stage.tile([P, S], F32, name="folded%d" % b, offset=STAGED[min(b, 3)])
+                folded = stage.tile([P, S], F32, name="folded%d" % b, offset=FOLDED_AT[min(b, 3)])
                 for half in range(S // BANK):
                     fold(b, folded[:, BANK * half : BANK * (half + 1)], BANK * half, BANK, banks[2 * (b % 2) + half])
                 if b < FOLDED:
@@ -265,10 +267,8 @@ def tile_list_birdsong_retrieval_kernel(
             woven[a, q] = tile
 
         for b in range(AHEAD):
-            if b < 2:
-                quantise_w1(b + 1)
             phases(b)
-        quantise_w1(len(W1_LOADS) - 1)
+            quantise_w1(b + 1)
         floor = keep.tile([P, CALL_TILES], F32, name="floor")
         tab2_tiles = []
         for b in range(ROW_TILES):
@@ -312,8 +312,8 @@ def tile_list_birdsong_retrieval_kernel(
             nc.vector.quantize_mx(out=codes[:].bitcast(FP8X4), scales=scales[:], in_=woven[1, q].bitcast(BF16))
             page_codes[1, q] = (codes[:], scales[:])
 
-        call_codes.append(shelf.tile([P, S2], U32, name="call_codes0", align_bytes=64, offset=FOLDED * 4 * S))
-        late_scales = shelf.tile([P, T2], U8, name="late_scales", align_bytes=64, offset=FOLDED * 4 * S + 4 * S2)
+        call_codes.append(shelf.tile([P, S2], U32, name="call_codes0", align_bytes=64, offset=WGS_AT))
+        late_scales = shelf.tile([P, T2], U8, name="late_scales", align_bytes=64, offset=WGS_AT + 4 * S2)
         gather_call_words(0, 0)
         for i in range(CHUNKS // 2):
             quantise_lower(i)

@@ -37,6 +37,7 @@ FOLDED_AT = {1: 4096, 2: 6144, 3: 12288}
 GROUPED_AT = {1: 16384, 2: 4096, 3: 6144}
 FIRST_FOLD = 4 * PACK * H
 FOLDED = 2
+W4_LOADS = ((0, 256), (256, 1024))
 PAGES = 5
 WGS_AT = 4 * max(FOLDED * S, PASSES * T3)
 SQUARE_ON_GPSIMD = 2
@@ -100,6 +101,15 @@ def tile_list_birdsong_retrieval_kernel(
             nc.sync.dma_start(out=raw[:], in_=w1[:, lo:hi].rearrange("(p j) c -> p j c", j=PACK))
             w1_raw.append(raw)
 
+        w4_codes = {}
+
+        def load_w4(i):
+            lo, hi = W4_LOADS[i]
+            words = keep.tile([P, 2 * (hi - lo)], U8, name="w4_words%d" % i, align_bytes=64)
+            nc.sync.dma_start(out=words[:].bitcast(I32), in_=w4_words[0, :, 2 * lo : 2 * hi].bitcast(I32))
+            for c0 in range(lo, hi, P):
+                w4_codes[c0 // P] = words[:, 2 * (c0 - lo) : 2 * (c0 - lo + P)]
+
         pages = []
 
         def load_page(b):
@@ -115,13 +125,13 @@ def tile_list_birdsong_retrieval_kernel(
         nc.sync.dma_start(out=tab2_rows[0:P:4, :].bitcast(I32), in_=tab2_scales.rearrange("a q t -> (a q) t").bitcast(I32))
         tab_tile = slab.tile([P, T], U32, name="tab_tile", align_bytes=64, offset=0)
         nc.sync.dma_start(out=tab_tile[:].bitcast(I32), in_=tab_words[0].rearrange("p t i -> p (t i)").bitcast(I32))
-        w4_tile = keep.tile([P, 2 * H], U8, name="w4_tile", align_bytes=64)
-        nc.sync.dma_start(out=w4_tile[:].bitcast(I32), in_=w4_words[0].bitcast(I32))
+        load_w4(0)
         load_plane(w4_plane, w4_scales)
         wgs_tile = shelf.tile([P, S], F32, name="wgs_tile", align_bytes=64, offset=WGS_AT)
         nc.sync.dma_start(out=wgs_tile[:], in_=wgs)
         load_page(0)
         load_w1(1)
+        load_w4(1)
         load_page(1)
         load_w1(2)
         load_w1(3)
@@ -187,7 +197,7 @@ def tile_list_birdsong_retrieval_kernel(
             moving, moving_scale = v_codes[half][:, c0 : c0 + width].bitcast(FP8X4), v_scales[half][:, c0 : c0 + width]
             codes, scales = w1_codes[b]
             nc.tensor.matmul_mx(
-                out=acc[:, 0:width], lhsT=w4_tile[:, 2 * P * b : 2 * P * (b + 1)].bitcast(FP4X4),
+                out=acc[:, 0:width], lhsT=w4_codes[b].bitcast(FP4X4),
                 lhsT_scale=w4_plane[:, P * b : P * (b + 1)], rhs=moving, rhs_scale=moving_scale, start=True, stop=False,
             )
             nc.tensor.matmul_mx(
@@ -223,7 +233,7 @@ def tile_list_birdsong_retrieval_kernel(
         def scatter(b):
             wave = waves[b]
             factor = weights[b] if b < FOLDED else wgs_tile
-            for first, width in FIRST_PIECES if b == 0 else ((0, S),):
+            for first, width in ((0, PIECE), (PIECE, S - PIECE)) if b == 0 else ((0, S),):
                 cols = slice(first, first + width)
                 nc.vector.tensor_tensor(
                     pages[b][:].indirect(part_of(place_list, first, width)), wave[:, cols], factor[:, cols], ALU.mult
@@ -358,7 +368,7 @@ def tile_list_birdsong_retrieval_kernel(
                 nc.gpsimd.tensor_tensor(result[:], picked[:], picked[:], ALU.mult)
             elif piece < len(pieces) - 1:
                 result = keep.tile([P, width], F32, name="result", tag="codes%d" % spare_tags.pop(), align_bytes=64)
-                if width == BANK:
+                if n < CALL_TILES - 1:
                     nc.gpsimd.tensor_scalar(picked[:], picked[:], FLOAT_MAX, bound, ALU.min, ALU.max)
                 else:
                     nc.vector.tensor_scalar(picked[:], picked[:], bound, None, ALU.max)

@@ -27,22 +27,25 @@ PASSES = H // (P * PACK)
 CHUNKS = T2 // BANK
 CALL_TILES = S2 // P
 HALF_CALLS = S2 // 2
-LAST = ROW_TILES - 1
-W1_LOADS = ((0, 256), (256, 512), (512, 768), (768, 1024))
-AHEAD = 3
+FLOAT_MAX = 3.4028234663852886e38
+
 PIECE = 256
-FIRST_PIECES = ((0, PIECE), (PIECE, PIECE), (BANK, BANK))
-LOWER_BACK = {4: (0,), 5: (1,), 6: (2, 3)}
-FOLDED_AT = {1: 4096, 2: 6144, 3: 12288}
-GROUPED_AT = {1: 16384, 2: 4096, 3: 6144}
-FIRST_FOLD = 4 * PACK * H
-FOLDED = 2
-W4_LOADS = ((0, 256), (256, 1024))
+AHEAD = 3
 PAGES = 5
-WGS_AT = 4 * max(FOLDED * S, PASSES * T3)
+FOLDED = 2
 SQUARE_ON_GPSIMD = 2
 VECTOR_CHUNK = 3
-FLOAT_MAX = 3.4028234663852886e38
+
+W1_LOADS = tuple((lo, lo + 2 * P) for lo in range(0, H, 2 * P))
+W4_LOADS = ((0, 2 * P), (2 * P, H))
+FIRST_PIECES = ((0, PIECE), (PIECE, PIECE), (BANK, BANK))
+LOWER_BACK = {PACK: (0,), PACK + 1: (1,), PACK + 2: (2, 3)}
+
+W1_SLICE = 4 * PACK * 2 * P
+FIRST_FOLD = len(W1_LOADS) * W1_SLICE
+FOLD_AT = {1: W1_SLICE, 2: W1_SLICE + W1_SLICE // 2, 3: 3 * W1_SLICE}
+CAST_AT = {1: FIRST_FOLD, 2: W1_SLICE, 3: W1_SLICE + W1_SLICE // 2}
+WGS_AT = 4 * max(FOLDED * S, PASSES * T3)
 
 
 def tile_list_birdsong_retrieval_kernel(
@@ -67,15 +70,15 @@ def tile_list_birdsong_retrieval_kernel(
         def part_of(list_tile, first, count):
             return list_tile[:, first // STRIPE : (first + count) // STRIPE]
 
-        def load_plane(plane, source):
+        def load_scale_rows(tile, source):
             rows = source[0].rearrange("(quad r) c -> r quad c", r=4)
             for r in range(4):
-                nc.sync.dma_start(out=plane[r:P:32, :].bitcast(I32), in_=rows[r].bitcast(I32))
+                nc.sync.dma_start(out=tile[r:P:32, :].bitcast(I32), in_=rows[r].bitcast(I32))
 
-        tab_plane = keep.tile([P, T], U8, name="tab_plane", align_bytes=64)
-        nc.vector.memset(tab_plane[:].bitcast(I32), 0)
-        w4_plane = keep.tile([P, H], U8, name="w4_plane", align_bytes=64)
-        nc.vector.memset(w4_plane[:].bitcast(I32), 0)
+        tab_scale_tile = keep.tile([P, T], U8, name="tab_scale_tile", align_bytes=64)
+        nc.vector.memset(tab_scale_tile[:].bitcast(I32), 0)
+        w4_scale_tile = keep.tile([P, H], U8, name="w4_scale_tile", align_bytes=64)
+        nc.vector.memset(w4_scale_tile[:].bitcast(I32), 0)
         zero = keep.tile([P, 1], F32, name="zero")
         nc.vector.memset(zero[:], 0.0)
         half_amp = keep.tile([P, 1], F32, name="half_amp")
@@ -121,12 +124,12 @@ def tile_list_birdsong_retrieval_kernel(
         call_list = load_list("call_list", offs2)
         place_list = load_list("place_list", offs3)
         load_w1(0)
-        load_plane(tab_plane, tab_scales)
+        load_scale_rows(tab_scale_tile, tab_scales)
         nc.sync.dma_start(out=tab2_rows[0:P:4, :].bitcast(I32), in_=tab2_scales.rearrange("a q t -> (a q) t").bitcast(I32))
         tab_tile = slab.tile([P, T], U32, name="tab_tile", align_bytes=64, offset=0)
         nc.sync.dma_start(out=tab_tile[:].bitcast(I32), in_=tab_words[0].rearrange("p t i -> p (t i)").bitcast(I32))
         load_w4(0)
-        load_plane(w4_plane, w4_scales)
+        load_scale_rows(w4_scale_tile, w4_scales)
         wgs_tile = shelf.tile([P, S], F32, name="wgs_tile", align_bytes=64, offset=WGS_AT)
         nc.sync.dma_start(out=wgs_tile[:], in_=wgs)
         load_page(0)
@@ -136,9 +139,8 @@ def tile_list_birdsong_retrieval_kernel(
         load_w1(2)
         load_w1(3)
         nc.sync.dma_start(out=low_rows[0:CALL_TILES, :], in_=low.rearrange("(n p) -> n p", p=P))
-        load_page(2)
-        load_page(3)
-        load_page(4)
+        for b in range(2, PAGES):
+            load_page(b)
         read_list = load_list("read_list", offs4)
 
         banks = [psum.tile([P, BANK], F32, name="bank%d" % i) for i in range(8)]
@@ -149,7 +151,7 @@ def tile_list_birdsong_retrieval_kernel(
         v_codes, v_scales = [], []
         for half in range(S // BANK):
             scales = keep.tile([P, BANK], U8, name="v_scales%d" % half, align_bytes=64)
-            nc.vector.tensor_copy(scales[:], tab_plane[:].indirect(part_of(clip_list, BANK * half, BANK)))
+            nc.vector.tensor_copy(scales[:], tab_scale_tile[:].indirect(part_of(clip_list, BANK * half, BANK)))
             v_scales.append(scales)
         call_rows = keep.tile([P, S2], U8, name="call_rows", align_bytes=64)
         nc.vector.tensor_copy(call_rows[:], tab2_rows[:].indirect(call_list[:]))
@@ -167,7 +169,7 @@ def tile_list_birdsong_retrieval_kernel(
             if load == 0:
                 grouped = keep.tile([P, (hi - lo) * PACK], BF16, name="w1_grouped%d" % lo, align_bytes=64)
             else:
-                grouped = stage.tile([P, (hi - lo) * PACK], BF16, name="w1_grouped%d" % lo, align_bytes=64, offset=GROUPED_AT[load])
+                grouped = stage.tile([P, (hi - lo) * PACK], BF16, name="w1_grouped%d" % lo, align_bytes=64, offset=CAST_AT[load])
             nc.scalar.copy(
                 out=grouped[:].rearrange("p (c i j) -> p c j i", i=4, j=PACK),
                 in_=w1_raw[load][:].rearrange("p j (c i) -> p c j i", i=4),
@@ -186,9 +188,9 @@ def tile_list_birdsong_retrieval_kernel(
 
         weights = []
         for b in range(FOLDED):
-            folded_weights = shelf.tile([P, S], F32, name="weights%d" % b, align_bytes=64, offset=4 * S * b)
-            nc.vector.tensor_scalar(folded_weights[:], wgs_tile[:], amp_gain[:, b : b + 1], None, ALU.mult)
-            weights.append(folded_weights)
+            scaled_wgs = shelf.tile([P, S], F32, name="weights%d" % b, align_bytes=64, offset=4 * S * b)
+            nc.vector.tensor_scalar(scaled_wgs[:], wgs_tile[:], amp_gain[:, b : b + 1], None, ALU.mult)
+            weights.append(scaled_wgs)
 
         waves = {}
 
@@ -198,7 +200,7 @@ def tile_list_birdsong_retrieval_kernel(
             codes, scales = w1_codes[b]
             nc.tensor.matmul_mx(
                 out=acc[:, 0:width], lhsT=w4_codes[b].bitcast(FP4X4),
-                lhsT_scale=w4_plane[:, P * b : P * (b + 1)], rhs=moving, rhs_scale=moving_scale, start=True, stop=False,
+                lhsT_scale=w4_scale_tile[:, P * b : P * (b + 1)], rhs=moving, rhs_scale=moving_scale, start=True, stop=False,
             )
             nc.tensor.matmul_mx(
                 out=acc[:, 0:width], lhsT=codes.bitcast(FP8X4), lhsT_scale=scales,
@@ -206,8 +208,8 @@ def tile_list_birdsong_retrieval_kernel(
             )
             nc.scalar.activation(out=folded, in_=acc[:, 0:width], func=ACT.Abs, bias=-math.pi / 4)
 
-        def cosine(unit, folded):
-            nc.scalar.activation(out=unit, in_=folded, func=ACT.Sin, scale=-1.0, bias=math.pi / 2)
+        def cosine(target, folded):
+            nc.scalar.activation(out=target, in_=folded, func=ACT.Sin, scale=-1.0, bias=math.pi / 2)
 
         def phases(b):
             wave = ring.tile([P, S], F32, name="wave", tag="wave", bufs=AHEAD + 2)
@@ -220,7 +222,7 @@ def tile_list_birdsong_retrieval_kernel(
                     fold(b, folded[:], first, width, banks[4 + piece])
                     cosine(wave[:, first : first + width], folded[:])
             else:
-                folded = stage.tile([P, S], F32, name="folded%d" % b, offset=FOLDED_AT[min(b, 3)])
+                folded = stage.tile([P, S], F32, name="folded%d" % b, offset=FOLD_AT[min(b, max(FOLD_AT))])
                 for half in range(S // BANK):
                     fold(b, folded[:, BANK * half : BANK * (half + 1)], BANK * half, BANK, banks[2 * (b % 2) + half])
                 if b < FOLDED:
@@ -310,7 +312,7 @@ def tile_list_birdsong_retrieval_kernel(
             )
 
         def quantise_lower(i):
-            scales = late_scales[:, 2 * BANK * i : 2 * BANK * (i + 1)]
+            scales = lower_scales[:, 2 * BANK * i : 2 * BANK * (i + 1)]
             codes = keep.tile([P, 2 * BANK], U32, name="lower_codes", tag="codes%d" % i, align_bytes=64)
             nc.vector.quantize_mx(out=codes[:].bitcast(FP8X4), scales=scales, in_=lower_woven[i][:].bitcast(BF16))
             for k in range(2):
@@ -323,25 +325,29 @@ def tile_list_birdsong_retrieval_kernel(
             page_codes[1, q] = (codes[:], scales[:])
 
         call_codes.append(shelf.tile([P, S2], U32, name="call_codes0", align_bytes=64, offset=WGS_AT))
-        late_scales = shelf.tile([P, T2], U8, name="late_scales", align_bytes=64, offset=WGS_AT + 4 * S2)
+        lower_scales = shelf.tile([P, T2], U8, name="lower_scales", align_bytes=64, offset=WGS_AT + 4 * S2)
         gather_call_words(0, 0)
         for i in range(CHUNKS // 2):
             quantise_lower(i)
         gather_call_words(0, 1)
-        order = (0, VECTOR_CHUNK, 1, 2)
+        order = [q for q in range(CHUNKS) if q != VECTOR_CHUNK]
+        order.insert(1, VECTOR_CHUNK)
         for place, q in enumerate(order):
-            turn_back(1, q, 4 + 2 * (place % 2), nc.vector.tensor_copy if q == VECTOR_CHUNK else nc.scalar.copy)
+            turn_back(1, q, (4 + 2 * place) % 8, nc.vector.tensor_copy if q == VECTOR_CHUNK else nc.scalar.copy)
         for q in order:
             quantise_upper(q)
         call_codes.append(keep.tile([P, S2], U32, name="call_codes1", tag="turned%d" % order[-1], align_bytes=64))
         for a in range(PASSES):
             gather_call_words(1, a)
 
+        def score_bank(n, q):
+            return banks[(CHUNKS * (n + 1) + order.index(q)) % 8]
+
         def product(n, q, a):
             codes, scales = page_codes[a, q]
             half, c0 = n // 2, P * (n % 2)
             nc.tensor.matmul_mx(
-                out=banks[(CHUNKS * n + q) % 8][:],
+                out=score_bank(n, q)[:],
                 lhsT=call_codes[half][:, HALF_CALLS * a + c0 : HALF_CALLS * a + c0 + P].bitcast(FP8X4),
                 lhsT_scale=call_scales[4 * a : P, P * n : P * (n + 1)],
                 rhs=codes.bitcast(FP8X4), rhs_scale=scales, start=(a == 0), stop=(a == PASSES - 1),
@@ -353,7 +359,7 @@ def tile_list_birdsong_retrieval_kernel(
                 if n > 0:
                     product(n, q, 0)
                 product(n, q, 1)
-                nc.scalar.copy(out=e[:, BANK * q : BANK * (q + 1)], in_=banks[(CHUNKS * n + q) % 8][:])
+                nc.scalar.copy(out=e[:, BANK * q : BANK * (q + 1)], in_=score_bank(n, q)[:])
             return e
 
         spare_tags = list(range(CHUNKS // 2 + CHUNKS))

@@ -33,8 +33,9 @@ PIECE = 256
 AHEAD = 3
 PAGES = 5
 FOLDED = 2
-SQUARE_ON_GPSIMD = 2
+SQUARE_ON_GPSIMD = 1
 VECTOR_CHUNK = 3
+ORDER = (0, VECTOR_CHUNK, 1, 2)
 
 W1_LOADS = tuple((lo, lo + 2 * P) for lo in range(0, H, 2 * P))
 W4_LOADS = ((0, 2 * P), (2 * P, H))
@@ -45,6 +46,11 @@ W1_SLICE = 4 * PACK * 2 * P
 FIRST_FOLD = len(W1_LOADS) * W1_SLICE
 FOLD_AT = {1: W1_SLICE, 2: W1_SLICE + W1_SLICE // 2, 3: 3 * W1_SLICE}
 CAST_AT = {1: FIRST_FOLD, 2: W1_SLICE, 3: W1_SLICE + W1_SLICE // 2}
+SLOT = 2 * PACK * BANK
+LAST_CALLS = CHUNKS * SLOT - 4 * S2
+LAST_CODES = CHUNKS * SLOT
+LAST_SCALES = LAST_CODES + 4 * BANK
+CALL_SCALES = LAST_SCALES + BANK
 WGS_AT = 4 * max(FOLDED * S, PASSES * T3)
 
 
@@ -60,6 +66,7 @@ def tile_list_birdsong_retrieval_kernel(
         slab = ctx.enter_context(tc.tile_pool(name="slab", bufs=1))
         shelf = ctx.enter_context(tc.tile_pool(name="shelf", bufs=1))
         stage = ctx.enter_context(tc.tile_pool(name="stage", bufs=1))
+        late = ctx.enter_context(tc.tile_pool(name="late", bufs=1))
         psum = ctx.enter_context(tc.psum_pool(name="psum", bufs=1))
 
         def load_list(name, source):
@@ -91,7 +98,7 @@ def tile_list_birdsong_retrieval_kernel(
         nc.gpsimd.dma_start(out=gain_rows[0:ROW_TILES, :], in_=gain.rearrange("(b p) -> b p", p=P))
         ident = keep.tile([P, P], F32, name="ident")
         make_identity(nc, ident[:])
-        call_scales = keep.tile([P, S2], U8, name="call_scales", align_bytes=64)
+        call_scales = late.tile([P, S2], U8, name="call_scales", align_bytes=64, offset=CALL_SCALES)
         nc.gpsimd.memset(call_scales[:].bitcast(I32), 0)
         low_rows = keep.tile([P, P], F32, name="low_rows")
         nc.gpsimd.memset(low_rows[:], 0.0)
@@ -182,9 +189,10 @@ def tile_list_birdsong_retrieval_kernel(
 
         quantise_w1(0)
         for half in range(S // BANK):
-            codes = keep.tile([P, BANK], U32, name="v_codes%d" % half, align_bytes=64)
-            nc.vector.tensor_copy(codes[:], tab_tile[:].indirect(part_of(clip_list, BANK * half, BANK)))
-            v_codes.append(codes)
+            v_codes.append(keep.tile([P, BANK], U32, name="v_codes%d" % half, align_bytes=64))
+        for first, width in FIRST_PIECES:
+            half, c0 = divmod(first, BANK)
+            nc.vector.tensor_copy(v_codes[half][:, c0 : c0 + width], tab_tile[:].indirect(part_of(clip_list, first, width)))
 
         weights = []
         for b in range(FOLDED):
@@ -246,7 +254,7 @@ def tile_list_birdsong_retrieval_kernel(
         def turn_page(b, q):
             a, quad = divmod(b, PACK)
             if b == 0:
-                turned[a, q] = keep.tile([P, PACK * BANK], BF16, name="turned0", tag="turned%d" % q, align_bytes=64)
+                turned[a, q] = late.tile([P, PACK * BANK], BF16, name="turned0_%d" % q, align_bytes=64, offset=SLOT * ORDER.index(q))
             elif b == PACK:
                 turned[a, q] = slab.tile([P, PACK * BANK], BF16, name="turned1_%d" % q, align_bytes=64, offset=2 * PACK * BANK * q)
             bank = banks[2 * ((b + AHEAD) % 2) + q % 2 if b + AHEAD < ROW_TILES else q]
@@ -265,7 +273,7 @@ def tile_list_birdsong_retrieval_kernel(
             if a == 0:
                 tile = lower_woven[q // 2][:, 2 * BANK * (q % 2) : 2 * BANK * (q % 2 + 1)]
             else:
-                tile = keep.tile([P, 2 * BANK], F32, name="woven1", tag="turned%d" % q, align_bytes=64)[:]
+                tile = late.tile([P, 2 * BANK], F32, name="woven1_%d" % q, align_bytes=64, offset=SLOT * ORDER.index(q))[:]
             words = turned[a, q][:].bitcast(F32)
             for k in range(2):
                 bank = banks[first_bank + k]
@@ -313,14 +321,18 @@ def tile_list_birdsong_retrieval_kernel(
 
         def quantise_lower(i):
             scales = lower_scales[:, 2 * BANK * i : 2 * BANK * (i + 1)]
-            codes = keep.tile([P, 2 * BANK], U32, name="lower_codes", tag="codes%d" % i, align_bytes=64)
+            codes = keep.tile([P, 2 * BANK], U32, name="lower_codes%d" % i, align_bytes=64)
             nc.vector.quantize_mx(out=codes[:].bitcast(FP8X4), scales=scales, in_=lower_woven[i][:].bitcast(BF16))
             for k in range(2):
                 page_codes[0, 2 * i + k] = (codes[:, BANK * k : BANK * (k + 1)], scales[:, BANK * k : BANK * (k + 1)])
 
         def quantise_upper(q):
-            scales = keep.tile([P, BANK], U8, name="upper_scales%d" % q, align_bytes=64)
-            codes = keep.tile([P, BANK], U32, name="upper_codes", tag="codes%d" % (2 + q), align_bytes=64)
+            if q == ORDER[-1]:
+                scales = late.tile([P, BANK], U8, name="last_scales", align_bytes=64, offset=LAST_SCALES)
+                codes = late.tile([P, BANK], U32, name="last_codes", align_bytes=64, offset=LAST_CODES)
+            else:
+                scales = keep.tile([P, BANK], U8, name="upper_scales%d" % q, align_bytes=64)
+                codes = keep.tile([P, BANK], U32, name="upper_codes%d" % q, align_bytes=64)
             nc.vector.quantize_mx(out=codes[:].bitcast(FP8X4), scales=scales[:], in_=woven[1, q].bitcast(BF16))
             page_codes[1, q] = (codes[:], scales[:])
 
@@ -330,18 +342,16 @@ def tile_list_birdsong_retrieval_kernel(
         for i in range(CHUNKS // 2):
             quantise_lower(i)
         gather_call_words(0, 1)
-        order = [q for q in range(CHUNKS) if q != VECTOR_CHUNK]
-        order.insert(1, VECTOR_CHUNK)
-        for place, q in enumerate(order):
+        for place, q in enumerate(ORDER):
             turn_back(1, q, (4 + 2 * place) % 8, nc.vector.tensor_copy if q == VECTOR_CHUNK else nc.scalar.copy)
-        for q in order:
+        for q in ORDER:
             quantise_upper(q)
-        call_codes.append(keep.tile([P, S2], U32, name="call_codes1", tag="turned%d" % order[-1], align_bytes=64))
+        call_codes.append(late.tile([P, S2], U32, name="call_codes1", align_bytes=64, offset=LAST_CALLS))
         for a in range(PASSES):
             gather_call_words(1, a)
 
         def score_bank(n, q):
-            return banks[(CHUNKS * (n + 1) + order.index(q)) % 8]
+            return banks[(CHUNKS * (n + 1) + ORDER.index(q)) % 8]
 
         def product(n, q, a):
             codes, scales = page_codes[a, q]
@@ -355,14 +365,12 @@ def tile_list_birdsong_retrieval_kernel(
 
         def scores(n):
             e = ring.tile([P, T2], F32, name="e", tag="rows", bufs=PAGES)
-            for q in order:
-                if n > 0:
-                    product(n, q, 0)
-                product(n, q, 1)
+            for q in ORDER:
+                for a in range(PASSES):
+                    product(n, q, a)
                 nc.scalar.copy(out=e[:, BANK * q : BANK * (q + 1)], in_=score_bank(n, q)[:])
             return e
 
-        spare_tags = list(range(CHUNKS // 2 + CHUNKS))
 
         def finish(piece, n, first, width, e):
             picked = keep.tile([P, width], F32, name="picked%d" % piece)
@@ -373,11 +381,9 @@ def tile_list_birdsong_retrieval_kernel(
                 nc.gpsimd.tensor_scalar(picked[:], picked[:], FLOAT_MAX, bound, ALU.min, ALU.max)
                 nc.gpsimd.tensor_tensor(result[:], picked[:], picked[:], ALU.mult)
             elif piece < len(pieces) - 1:
-                result = keep.tile([P, width], F32, name="result", tag="codes%d" % spare_tags.pop(), align_bytes=64)
-                if n < CALL_TILES - 1:
-                    nc.gpsimd.tensor_scalar(picked[:], picked[:], FLOAT_MAX, bound, ALU.min, ALU.max)
-                else:
-                    nc.vector.tensor_scalar(picked[:], picked[:], bound, None, ALU.max)
+                at = LAST_CALLS + 64 + 4 * BANK * (piece - SQUARE_ON_GPSIMD - 1)
+                result = late.tile([P, width], F32, name="result%d" % piece, align_bytes=64, offset=at)
+                nc.gpsimd.tensor_scalar(picked[:], picked[:], FLOAT_MAX, bound, ALU.min, ALU.max)
                 nc.scalar.activation(out=result[:], in_=picked[:], func=ACT.Square)
             else:
                 result = keep.tile([P, width], F32, name="result%d" % piece)
@@ -385,10 +391,8 @@ def tile_list_birdsong_retrieval_kernel(
                 nc.vector.tensor_tensor(result[:], picked[:], picked[:], ALU.mult)
             nc.sync.dma_start(out=out[P * n : P * (n + 1), first : first + width], in_=result[:])
 
-        for q in range(CHUNKS):
-            product(0, q, 0)
         score_tiles = [scores(n) for n in range(CALL_TILES)]
         pieces = [(n, first, BANK) for n in range(CALL_TILES) for first in range(0, PICKS, BANK)]
-        pieces = pieces[:-1] + [(CALL_TILES - 1, BANK, PIECE), (CALL_TILES - 1, BANK + PIECE, PIECE)]
+        pieces = pieces[:-1] + [(CALL_TILES - 1, BANK, BANK - P), (CALL_TILES - 1, PICKS - P, P)]
         for piece, (n, first, width) in enumerate(pieces):
             finish(piece, n, first, width, score_tiles[n])

@@ -82,16 +82,20 @@ def tile_list_birdsong_retrieval_kernel(
             for r in range(4):
                 nc.sync.dma_start(out=tile[r:P:32, :].bitcast(I32), in_=rows[r].bitcast(I32))
 
-        tab_scale_tile = keep.tile([P, T], U8, name="tab_scale_tile", align_bytes=64)
-        nc.vector.memset(tab_scale_tile[:].bitcast(I32), 0)
-        w4_scale_tile = keep.tile([P, H], U8, name="w4_scale_tile", align_bytes=64)
-        nc.vector.memset(w4_scale_tile[:].bitcast(I32), 0)
+        tab_rows = keep.tile([P, T], U8, name="tab_rows", align_bytes=64)
+        nc.vector.memset(tab_rows[:].bitcast(I32), 0)
         zero = keep.tile([P, 1], F32, name="zero")
         nc.vector.memset(zero[:], 0.0)
         half_amp = keep.tile([P, 1], F32, name="half_amp")
         nc.scalar.activation(out=half_amp[:], in_=zero[:], func=ACT.Sin, bias=math.pi / 4)
         tab2_rows = keep.tile([P, T3], U8, name="tab2_rows", align_bytes=64)
         nc.vector.memset(tab2_rows[:].bitcast(I32), 0)
+        w4_scale_tile = keep.tile([P, H], U8, name="w4_scale_tile", align_bytes=64)
+        nc.vector.memset(w4_scale_tile[:].bitcast(I32), 0)
+        v_scales = keep.tile([P, S], U8, name="v_scales", align_bytes=64)
+        nc.vector.memset(v_scales[:].bitcast(I32), 0)
+        low_rows = keep.tile([P, P], F32, name="low_rows")
+        nc.vector.memset(low_rows[:], 0.0)
 
         gain_rows = keep.tile([P, P], F32, name="gain_rows")
         nc.gpsimd.memset(gain_rows[:], 0.0)
@@ -100,8 +104,6 @@ def tile_list_birdsong_retrieval_kernel(
         make_identity(nc, ident[:])
         call_scales = late.tile([P, S2], U8, name="call_scales", align_bytes=64, offset=CALL_SCALES)
         nc.gpsimd.memset(call_scales[:].bitcast(I32), 0)
-        low_rows = keep.tile([P, P], F32, name="low_rows")
-        nc.gpsimd.memset(low_rows[:], 0.0)
 
         w1_raw = []
 
@@ -130,13 +132,18 @@ def tile_list_birdsong_retrieval_kernel(
         clip_list = load_list("clip_list", offs)
         call_list = load_list("call_list", offs2)
         place_list = load_list("place_list", offs3)
+        load_w4(0)
+        nc.sync.dma_start(out=tab_rows[0:P:8, :].bitcast(I32), in_=tab_scales[0].bitcast(I32))
         load_w1(0)
-        load_scale_rows(tab_scale_tile, tab_scales)
         nc.sync.dma_start(out=tab2_rows[0:P:4, :].bitcast(I32), in_=tab2_scales.rearrange("a q t -> (a q) t").bitcast(I32))
+        load_scale_rows(w4_scale_tile, w4_scales)
         tab_tile = slab.tile([P, T], U32, name="tab_tile", align_bytes=64, offset=0)
         nc.sync.dma_start(out=tab_tile[:].bitcast(I32), in_=tab_words[0].rearrange("p t i -> p (t i)").bitcast(I32))
-        load_w4(0)
-        load_scale_rows(w4_scale_tile, w4_scales)
+        read_list = load_list("read_list", offs4)
+        clip_rows = keep.tile([P, S], U8, name="clip_rows", align_bytes=64)
+        nc.vector.tensor_copy(clip_rows[:], tab_rows[:].indirect(clip_list[:]))
+        for r in range(4):
+            nc.sync.dma_start(out=v_scales[r:P:32, :].bitcast(I32), in_=clip_rows[8 * r : P : 32, :].bitcast(I32))
         wgs_tile = shelf.tile([P, S], F32, name="wgs_tile", align_bytes=64, offset=WGS_AT)
         nc.sync.dma_start(out=wgs_tile[:], in_=wgs)
         load_page(0)
@@ -148,18 +155,13 @@ def tile_list_birdsong_retrieval_kernel(
         nc.sync.dma_start(out=low_rows[0:CALL_TILES, :], in_=low.rearrange("(n p) -> n p", p=P))
         for b in range(2, PAGES):
             load_page(b)
-        read_list = load_list("read_list", offs4)
 
         banks = [psum.tile([P, BANK], F32, name="bank%d" % i) for i in range(8)]
         nc.tensor.transpose(banks[7][:, 0:P], gain_rows[:], ident[:])
         amp_gain = keep.tile([P, ROW_TILES], F32, name="amp_gain")
         nc.vector.tensor_scalar(amp_gain[:], banks[7][:, 0:ROW_TILES], half_amp[:], 2.0, ALU.mult, ALU.mult)
 
-        v_codes, v_scales = [], []
-        for half in range(S // BANK):
-            scales = keep.tile([P, BANK], U8, name="v_scales%d" % half, align_bytes=64)
-            nc.vector.tensor_copy(scales[:], tab_scale_tile[:].indirect(part_of(clip_list, BANK * half, BANK)))
-            v_scales.append(scales)
+        v_codes = []
         call_rows = keep.tile([P, S2], U8, name="call_rows", align_bytes=64)
         nc.vector.tensor_copy(call_rows[:], tab2_rows[:].indirect(call_list[:]))
         for a in range(PASSES):
@@ -204,7 +206,7 @@ def tile_list_birdsong_retrieval_kernel(
 
         def fold(b, folded, first, width, acc):
             half, c0 = divmod(first, BANK)
-            moving, moving_scale = v_codes[half][:, c0 : c0 + width].bitcast(FP8X4), v_scales[half][:, c0 : c0 + width]
+            moving, moving_scale = v_codes[half][:, c0 : c0 + width].bitcast(FP8X4), v_scales[:, first : first + width]
             codes, scales = w1_codes[b]
             nc.tensor.matmul_mx(
                 out=acc[:, 0:width], lhsT=w4_codes[b].bitcast(FP4X4),

@@ -77,10 +77,11 @@ def tile_list_birdsong_retrieval_kernel(
         def part_of(list_tile, first, count):
             return list_tile[:, first // STRIPE : (first + count) // STRIPE]
 
-        def load_scale_rows(tile, source):
-            rows = source[0].rearrange("(quad r) c -> r quad c", r=4)
+        def load_w4_scales(i):
+            lo, hi = W4_LOADS[i]
+            rows = w4_scales[0].rearrange("(quad r) c -> r quad c", r=4)
             for r in range(4):
-                nc.sync.dma_start(out=tile[r:P:32, :].bitcast(I32), in_=rows[r].bitcast(I32))
+                nc.sync.dma_start(out=w4_scale_tile[r:P:32, lo:hi].bitcast(I32), in_=rows[r, :, lo:hi].bitcast(I32))
 
         tab_rows = keep.tile([P, T], U8, name="tab_rows", align_bytes=64)
         nc.vector.memset(tab_rows[:].bitcast(I32), 0)
@@ -132,14 +133,14 @@ def tile_list_birdsong_retrieval_kernel(
         clip_list = load_list("clip_list", offs)
         call_list = load_list("call_list", offs2)
         place_list = load_list("place_list", offs3)
-        load_w4(0)
+        read_list = load_list("read_list", offs4)
         nc.sync.dma_start(out=tab_rows[0:P:8, :].bitcast(I32), in_=tab_scales[0].bitcast(I32))
         load_w1(0)
         nc.sync.dma_start(out=tab2_rows[0:P:4, :].bitcast(I32), in_=tab2_scales.rearrange("a q t -> (a q) t").bitcast(I32))
-        load_scale_rows(w4_scale_tile, w4_scales)
+        load_w4_scales(0)
         tab_tile = slab.tile([P, T], U32, name="tab_tile", align_bytes=64, offset=0)
         nc.sync.dma_start(out=tab_tile[:].bitcast(I32), in_=tab_words[0].rearrange("p t i -> p (t i)").bitcast(I32))
-        read_list = load_list("read_list", offs4)
+        load_w4(0)
         clip_rows = keep.tile([P, S], U8, name="clip_rows", align_bytes=64)
         nc.vector.tensor_copy(clip_rows[:], tab_rows[:].indirect(clip_list[:]))
         for r in range(4):
@@ -149,6 +150,7 @@ def tile_list_birdsong_retrieval_kernel(
         load_page(0)
         load_w1(1)
         load_w4(1)
+        load_w4_scales(1)
         load_page(1)
         load_w1(2)
         load_w1(3)

@@ -34,8 +34,8 @@ AHEAD = 3
 PAGES = 5
 FOLDED = 2
 SQUARE_ON_GPSIMD = 1
-VECTOR_CHUNK = 3
-ORDER = (0, VECTOR_CHUNK, 1, 2)
+VECTOR_CHUNK = 1
+ORDER = (0, VECTOR_CHUNK, 2, 3)
 
 W1_LOADS = tuple((lo, lo + 2 * P) for lo in range(0, H, 2 * P))
 W4_LOADS = ((0, 2 * P), (2 * P, H))

@@ -30,6 +30,7 @@ HALF_CALLS = S2 // 2
 FLOAT_MAX = 3.4028234663852886e38
 
 PIECE = 256
+LAST_PIECE = 192
 AHEAD = 3
 PAGES = 5
 FOLDED = 2
@@ -262,13 +263,15 @@ def tile_list_birdsong_retrieval_kernel(
             elif b == PACK:
                 turned[a, q] = slab.tile([P, PACK * BANK], BF16, name="turned1_%d" % q, align_bytes=64, offset=2 * PACK * BANK * q)
             bank = banks[2 * ((b + AHEAD) % 2) + q % 2 if b + AHEAD < ROW_TILES else q]
-            for i in range(4):
-                c0 = BANK * q + P * i
-                nc.tensor.transpose(bank[:, P * i : P * (i + 1)], pages[b][:, c0 : c0 + P], ident[:])
-            nc.scalar.copy(
-                out=turned[a, q][:].rearrange("c (i u p e) -> c i u p e", i=4, u=2, e=2)[:, :, :, 32 * quad : 32 * (quad + 1), :],
-                in_=bank[:].rearrange("c (i p u e) -> c i u p e", i=4, u=2, e=2),
-            )
+            target = turned[a, q][:].rearrange("c (i u p e) -> c i u p e", i=4, u=2, e=2)[:, :, :, 32 * quad : 32 * (quad + 1), :]
+            halves = ((bank, 0, 2), (banks[7], 2, 4)) if (b, q) == (ROW_TILES - 1, 0) else ((bank, 0, 4),)
+            for bank, lo, hi in halves:
+                for i in range(lo, hi):
+                    c0 = BANK * q + P * i
+                    nc.tensor.transpose(bank[:, P * i : P * (i + 1)], pages[b][:, c0 : c0 + P], ident[:])
+                nc.scalar.copy(
+                    out=target[:, lo:hi], in_=bank[:].rearrange("c (i p u e) -> c i u p e", i=4, u=2, e=2)[:, lo:hi]
+                )
 
         woven = {}
         lower_woven = [keep.tile([P, 4 * BANK], F32, name="woven0_%d" % i, align_bytes=64) for i in range(CHUNKS // 2)]
@@ -397,6 +400,6 @@ def tile_list_birdsong_retrieval_kernel(
 
         score_tiles = [scores(n) for n in range(CALL_TILES)]
         pieces = [(n, first, BANK) for n in range(CALL_TILES) for first in range(0, PICKS, BANK)]
-        pieces = pieces[:-1] + [(CALL_TILES - 1, BANK, BANK - P), (CALL_TILES - 1, PICKS - P, P)]
+        pieces = pieces[:-1] + [(CALL_TILES - 1, BANK, BANK - LAST_PIECE), (CALL_TILES - 1, PICKS - LAST_PIECE, LAST_PIECE)]
         for piece, (n, first, width) in enumerate(pieces):
             finish(piece, n, first, width, score_tiles[n])

import math
from contextlib import ExitStack

import concourse.mybir as mybir
from concourse.masks import make_identity

K, H, T, S, T2, T3, S2, PICKS = 512, 1024, 4096, 1024, 2048, 2048, 512, 1024
FLOPS = 2 * (2 * K * H * S + H * S2 * T2)

F32 = mybir.dt.float32
BF16 = mybir.dt.bfloat16
I32 = mybir.dt.int32
U32 = mybir.dt.uint32
U16 = mybir.dt.uint16
U8 = mybir.dt.uint8
FP8X4 = mybir.dt.float8_e4m3fn_x4
FP4X4 = mybir.dt.float4_e2m1fn_x4
ACT = mybir.ActivationFunctionType
ALU = mybir.AluOpType

P = 128
PACK = 4
BANK = 512
STRIPE = 16
ROW_TILES = H // P
PASSES = H // (P * PACK)
CHUNKS = T2 // BANK
CALL_TILES = S2 // P
HALF_CALLS = S2 // 2
FLOAT_MAX = 3.4028234663852886e38

PIECE = 256
LAST_PIECE = 192
AHEAD = 3
PAGES = 5
FOLDED = 2
SQUARE_ON_GPSIMD = 1
VECTOR_CHUNK = 1
ORDER = (0, VECTOR_CHUNK, 2, 3)

W1_LOADS = tuple((lo, lo + 2 * P) for lo in range(0, H, 2 * P))
W4_LOADS = ((0, 2 * P), (2 * P, H))
FIRST_PIECES = ((0, PIECE), (PIECE, PIECE), (BANK, BANK))
LOWER_BACK = {PACK: (0,), PACK + 1: (1,), PACK + 2: (2, 3)}

W1_SLICE = 4 * PACK * 2 * P
FIRST_FOLD = len(W1_LOADS) * W1_SLICE
FOLD_AT = {1: W1_SLICE, 2: W1_SLICE + W1_SLICE // 2, 3: 3 * W1_SLICE}
CAST_AT = {1: FIRST_FOLD, 2: W1_SLICE, 3: W1_SLICE + W1_SLICE // 2}
SLOT = 2 * PACK * BANK
LAST_CALLS = CHUNKS * SLOT - 4 * S2
LAST_CODES = CHUNKS * SLOT
LAST_SCALES = LAST_CODES + 4 * BANK
CALL_SCALES = LAST_SCALES + BANK
WGS_AT = 4 * max(FOLDED * S, PASSES * T3)


def tile_list_birdsong_retrieval_kernel(
    tc, tab_words, tab_scales, offs, tab2_words, tab2_scales, offs2, w4_words, w4_scales,
    w1, gain, page0, wgs, offs3, offs4, low, out,
):
    nc = tc.nc
    with ExitStack() as ctx:
        lists = ctx.enter_context(tc.tile_pool(name="lists", bufs=1))
        keep = ctx.enter_context(tc.tile_pool(name="keep", bufs=1))
        ring = ctx.enter_context(tc.tile_pool(name="ring", bufs=1))
        slab = ctx.enter_context(tc.tile_pool(name="slab", bufs=1))
        shelf = ctx.enter_context(tc.tile_pool(name="shelf", bufs=1))
        stage = ctx.enter_context(tc.tile_pool(name="stage", bufs=1))
        late = ctx.enter_context(tc.tile_pool(name="late", bufs=1))
        psum = ctx.enter_context(tc.psum_pool(name="psum", bufs=1))

        def load_list(name, source):
            tile = lists.tile(list(source.shape), U16, name=name)
            nc.sync.dma_start(tile[:], source)
            return tile

        def part_of(list_tile, first, count):
            return list_tile[:, first // STRIPE : (first + count) // STRIPE]

        def load_w4_scales(i):
            lo, hi = W4_LOADS[i]
            rows = w4_scales[0].rearrange("(quad r) c -> r quad c", r=4)
            for r in range(4):
                nc.sync.dma_start(out=w4_scale_tile[r:P:32, lo:hi].bitcast(I32), in_=rows[r, :, lo:hi].bitcast(I32))

        tab_rows = keep.tile([P, T], U8, name="tab_rows", align_bytes=64)
        nc.vector.memset(tab_rows[:].bitcast(I32), 0)
        zero = keep.tile([P, 1], F32, name="zero")
        nc.vector.memset(zero[:], 0.0)
        half_amp = keep.tile([P, 1], F32, name="half_amp")
        nc.scalar.activation(out=half_amp[:], in_=zero[:], func=ACT.Sin, bias=math.pi / 4)
        tab2_rows = keep.tile([P, T3], U8, name="tab2_rows", align_bytes=64)
        nc.vector.memset(tab2_rows[:].bitcast(I32), 0)
        w4_scale_tile = keep.tile([P, H], U8, name="w4_scale_tile", align_bytes=64)
        nc.vector.memset(w4_scale_tile[:].bitcast(I32), 0)
        v_scales = keep.tile([P, S], U8, name="v_scales", align_bytes=64)
        nc.vector.memset(v_scales[:].bitcast(I32), 0)
        low_rows = keep.tile([P, P], F32, name="low_rows")
        nc.vector.memset(low_rows[:], 0.0)

        gain_rows = keep.tile([P, P], F32, name="gain_rows")
        nc.gpsimd.memset(gain_rows[:], 0.0)
        nc.gpsimd.dma_start(out=gain_rows[0:ROW_TILES, :], in_=gain.rearrange("(b p) -> b p", p=P))
        ident = keep.tile([P, P], F32, name="ident")
        make_identity(nc, ident[:])
        call_scales = late.tile([P, S2], U8, name="call_scales", align_bytes=64, offset=CALL_SCALES)
        nc.gpsimd.memset(call_scales[:].bitcast(I32), 0)

        w1_raw = []

        def load_w1(i):
            lo, hi = W1_LOADS[i]
            raw = stage.tile([P, PACK, hi - lo], F32, name="w1_raw%d" % i, offset=4 * PACK * lo)
            nc.sync.dma_start(out=raw[:], in_=w1[:, lo:hi].rearrange("(p j) c -> p j c", j=PACK))
            w1_raw.append(raw)

        w4_codes = {}

        def load_w4(i):
            lo, hi = W4_LOADS[i]
            words = keep.tile([P, 2 * (hi - lo)], U8, name="w4_words%d" % i, align_bytes=64)
            nc.sync.dma_start(out=words[:].bitcast(I32), in_=w4_words[0, :, 2 * lo : 2 * hi].bitcast(I32))
            for c0 in range(lo, hi, P):
                w4_codes[c0 // P] = words[:, 2 * (c0 - lo) : 2 * (c0 - lo + P)]

        pages = []

        def load_page(b):
            page = ring.tile([P, T2], F32, name="page", tag="rows", bufs=PAGES)
            nc.sync.dma_start(out=page[:], in_=page0[P * b : P * (b + 1), :])
            pages.append(page)

        clip_list = load_list("clip_list", offs)
        call_list = load_list("call_list", offs2)
        place_list = load_list("place_list", offs3)
        read_list = load_list("read_list", offs4)
        nc.sync.dma_start(out=tab_rows[0:P:8, :].bitcast(I32), in_=tab_scales[0].bitcast(I32))
        load_w1(0)
        nc.sync.dma_start(out=tab2_rows[0:P:4, :].bitcast(I32), in_=tab2_scales.rearrange("a q t -> (a q) t").bitcast(I32))
        load_w4_scales(0)
        tab_tile = slab.tile([P, T], U32, name="tab_tile", align_bytes=64, offset=0)
        nc.sync.dma_start(out=tab_tile[:].bitcast(I32), in_=tab_words[0].rearrange("p t i -> p (t i)").bitcast(I32))
        load_w4(0)
        clip_rows = keep.tile([P, S], U8, name="clip_rows", align_bytes=64)
        nc.vector.tensor_copy(clip_rows[:], tab_rows[:].indirect(clip_list[:]))
        for r in range(4):
            nc.sync.dma_start(out=v_scales[r:P:32, :].bitcast(I32), in_=clip_rows[8 * r : P : 32, :].bitcast(I32))
        wgs_tile = shelf.tile([P, S], F32, name="wgs_tile", align_bytes=64, offset=WGS_AT)
        nc.sync.dma_start(out=wgs_tile[:], in_=wgs)
        load_page(0)
        load_w1(1)
        load_w4(1)
        load_w4_scales(1)
        load_page(1)
        load_w1(2)
        load_w1(3)
        nc.sync.dma_start(out=low_rows[0:CALL_TILES, :], in_=low.rearrange("(n p) -> n p", p=P))
        for b in range(2, PAGES):
            load_page(b)

        banks = [psum.tile([P, BANK], F32, name="bank%d" % i) for i in range(8)]
        nc.tensor.transpose(banks[7][:, 0:P], gain_rows[:], ident[:])
        amp_gain = keep.tile([P, ROW_TILES], F32, name="amp_gain")
        nc.vector.tensor_scalar(amp_gain[:], banks[7][:, 0:ROW_TILES], half_amp[:], 2.0, ALU.mult, ALU.mult)

        v_codes = []
        call_rows = keep.tile([P, S2], U8, name="call_rows", align_bytes=64)
        nc.vector.tensor_copy(call_rows[:], tab2_rows[:].indirect(call_list[:]))
        for a in range(PASSES):
            for r in range(4):
                nc.sync.dma_start(
                    out=call_scales[4 * a + r : P : 32, :].bitcast(I32),
                    in_=call_rows[64 * a + 4 * r : 64 * (a + 1) : 16, :].bitcast(I32),
                )

        w1_codes = {}

        def quantise_w1(load):
            lo, hi = W1_LOADS[load]
            if load == 0:
                grouped = keep.tile([P, (hi - lo) * PACK], BF16, name="w1_grouped%d" % lo, align_bytes=64)
            else:
                grouped = stage.tile([P, (hi - lo) * PACK], BF16, name="w1_grouped%d" % lo, align_bytes=64, offset=CAST_AT[load])
            nc.scalar.copy(
                out=grouped[:].rearrange("p (c i j) -> p c j i", i=4, j=PACK),
                in_=w1_raw[load][:].rearrange("p j (c i) -> p c j i", i=4),
            )
            codes = keep.tile([P, hi - lo], U32, name="w1_codes%d" % lo, align_bytes=64)
            scales = keep.tile([P, hi - lo], U8, name="w1_scales%d" % lo, align_bytes=64)
            nc.vector.quantize_mx(out=codes[:].bitcast(FP8X4), scales=scales[:], in_=grouped[:])
            for c0 in range(lo, hi, P):
                w1_codes[c0 // P] = (codes[:, c0 - lo : c0 - lo + P], scales[:, c0 - lo : c0 - lo + P])

        quantise_w1(0)
        for half in range(S // BANK):
            v_codes.append(keep.tile([P, BANK], U32, name="v_codes%d" % half, align_bytes=64))
        for first, width in FIRST_PIECES:
            half, c0 = divmod(first, BANK)
            nc.vector.tensor_copy(v_codes[half][:, c0 : c0 + width], tab_tile[:].indirect(part_of(clip_list, first, width)))

        weights = []
        for b in range(FOLDED):
            scaled_wgs = shelf.tile([P, S], F32, name="weights%d" % b, align_bytes=64, offset=4 * S * b)
            nc.vector.tensor_scalar(scaled_wgs[:], wgs_tile[:], amp_gain[:, b : b + 1], None, ALU.mult)
            weights.append(scaled_wgs)

        waves = {}

        def fold(b, folded, first, width, acc):
            half, c0 = divmod(first, BANK)
            moving, moving_scale = v_codes[half][:, c0 : c0 + width].bitcast(FP8X4), v_scales[:, first : first + width]
            codes, scales = w1_codes[b]
            nc.tensor.matmul_mx(
                out=acc[:, 0:width], lhsT=w4_codes[b].bitcast(FP4X4),
                lhsT_scale=w4_scale_tile[:, P * b : P * (b + 1)], rhs=moving, rhs_scale=moving_scale, start=True, stop=False,
            )
            nc.tensor.matmul_mx(
                out=acc[:, 0:width], lhsT=codes.bitcast(FP8X4), lhsT_scale=scales,
                rhs=moving, rhs_scale=moving_scale, start=False, stop=True,
            )
            nc.scalar.activation(out=folded, in_=acc[:, 0:width], func=ACT.Abs, bias=-math.pi / 4)

        def cosine(target, folded):
            nc.scalar.activation(out=target, in_=folded, func=ACT.Sin, scale=-1.0, bias=math.pi / 2)

        def phases(b):
            wave = ring.tile([P, S], F32, name="wave", tag="wave", bufs=AHEAD + 2)
            if b == 0:
                for piece, (first, width) in enumerate(FIRST_PIECES):
                    if width < BANK:
                        folded = ring.tile([P, width], F32, name="folded", tag="work", bufs=2)
                    else:
                        folded = stage.tile([P, width], F32, name="folded0", align_bytes=64, offset=FIRST_FOLD)
                    fold(b, folded[:], first, width, banks[4 + piece])
                    cosine(wave[:, first : first + width], folded[:])
            else:
                folded = stage.tile([P, S], F32, name="folded%d" % b, offset=FOLD_AT[min(b, max(FOLD_AT))])
                for half in range(S // BANK):
                    fold(b, folded[:, BANK * half : BANK * (half + 1)], BANK * half, BANK, banks[2 * (b % 2) + half])
                if b < FOLDED:
                    cosine(wave[:], folded[:])
                else:
                    cosine(folded[:], folded[:])
                    nc.scalar.activation(out=wave[:], in_=folded[:], func=ACT.Copy, scale=amp_gain[:, b : b + 1])
            waves[b] = wave

        def scatter(b):
            wave = waves[b]
            factor = weights[b] if b < FOLDED else wgs_tile
            for first, width in ((0, PIECE), (PIECE, S - PIECE)) if b == 0 else ((0, S),):
                cols = slice(first, first + width)
                nc.vector.tensor_tensor(
                    pages[b][:].indirect(part_of(place_list, first, width)), wave[:, cols], factor[:, cols], ALU.mult
                )

        turned = {}

        def turn_page(b, q):
            a, quad = divmod(b, PACK)
            if b == 0:
                turned[a, q] = late.tile([P, PACK * BANK], BF16, name="turned0_%d" % q, align_bytes=64, offset=SLOT * ORDER.index(q))
            elif b == PACK:
                turned[a, q] = slab.tile([P, PACK * BANK], BF16, name="turned1_%d" % q, align_bytes=64, offset=2 * PACK * BANK * q)
            bank = banks[2 * ((b + AHEAD) % 2) + q % 2 if b + AHEAD < ROW_TILES else q]
            target = turned[a, q][:].rearrange("c (i u p e) -> c i u p e", i=4, u=2, e=2)[:, :, :, 32 * quad : 32 * (quad + 1), :]
            halves = ((bank, 0, 2), (banks[7], 2, 4)) if (b, q) == (ROW_TILES - 1, 0) else ((bank, 0, 4),)
            for bank, lo, hi in halves:
                for i in range(lo, hi):
                    c0 = BANK * q + P * i
                    nc.tensor.transpose(bank[:, P * i : P * (i + 1)], pages[b][:, c0 : c0 + P], ident[:])
                nc.scalar.copy(
                    out=target[:, lo:hi], in_=bank[:].rearrange("c (i p u e) -> c i u p e", i=4, u=2, e=2)[:, lo:hi]
                )

        woven = {}
        lower_woven = [keep.tile([P, 4 * BANK], F32, name="woven0_%d" % i, align_bytes=64) for i in range(CHUNKS // 2)]

        def turn_back(a, q, first_bank, copy):
            if a == 0:
                tile = lower_woven[q // 2][:, 2 * BANK * (q % 2) : 2 * BANK * (q % 2 + 1)]
            else:
                tile = late.tile([P, 2 * BANK], F32, name="woven1_%d" % q, align_bytes=64, offset=SLOT * ORDER.index(q))[:]
            words = turned[a, q][:].bitcast(F32)
            for k in range(2):
                bank = banks[first_bank + k]
                for j in range(4):
                    c0 = BANK * k + P * j
                    nc.tensor.transpose(bank[:, P * j : P * (j + 1)], words[:, c0 : c0 + P], ident[:])
                copy(
                    out=tile[:, BANK * k : BANK * (k + 1)].rearrange("p (i c u) -> p i c u", i=2, u=2),
                    in_=bank[:].rearrange("p (i u c) -> p i c u", i=2, u=2),
                )
            woven[a, q] = tile

        for b in range(AHEAD):
            phases(b)
            quantise_w1(b + 1)
        floor = keep.tile([P, CALL_TILES], F32, name="floor")
        tab2_tiles = []
        for b in range(ROW_TILES):
            if b + AHEAD < ROW_TILES:
                phases(b + AHEAD)
            scatter(b)
            for q in LOWER_BACK.get(b, ()):
                turn_back(0, q, 4 + 2 * (q % 2), nc.scalar.copy)
            for q in range(CHUNKS):
                turn_page(b, q)
            if b == 1:
                nc.tensor.transpose(banks[0][:, 0:P], low_rows[:], ident[:])
                nc.scalar.copy(out=floor[:], in_=banks[0][:, 0:CALL_TILES])
            if b + PAGES < ROW_TILES:
                load_page(b + PAGES)
            if b == PACK - 1:
                for a in range(PASSES):
                    words = shelf.tile([P, T3], U32, name="tab2_tile%d" % a, align_bytes=64, offset=4 * T3 * a)
                    nc.sync.dma_start(out=words[:].bitcast(I32), in_=tab2_words[a].rearrange("p t i -> p (t i)").bitcast(I32))
                    tab2_tiles.append(words)

        call_codes = []
        page_codes = {}

        def gather_call_words(half, a):
            nc.vector.tensor_copy(
                call_codes[half][:, HALF_CALLS * a : HALF_CALLS * (a + 1)],
                tab2_tiles[a][:].indirect(part_of(call_list, HALF_CALLS * half, HALF_CALLS)),
            )

        def quantise_lower(i):
            scales = lower_scales[:, 2 * BANK * i : 2 * BANK * (i + 1)]
            codes = keep.tile([P, 2 * BANK], U32, name="lower_codes%d" % i, align_bytes=64)
            nc.vector.quantize_mx(out=codes[:].bitcast(FP8X4), scales=scales, in_=lower_woven[i][:].bitcast(BF16))
            for k in range(2):
                page_codes[0, 2 * i + k] = (codes[:, BANK * k : BANK * (k + 1)], scales[:, BANK * k : BANK * (k + 1)])

        def quantise_upper(q):
            if q == ORDER[-1]:
                scales = late.tile([P, BANK], U8, name="last_scales", align_bytes=64, offset=LAST_SCALES)
                codes = late.tile([P, BANK], U32, name="last_codes", align_bytes=64, offset=LAST_CODES)
            else:
                scales = keep.tile([P, BANK], U8, name="upper_scales%d" % q, align_bytes=64)
                codes = keep.tile([P, BANK], U32, name="upper_codes%d" % q, align_bytes=64)
            nc.vector.quantize_mx(out=codes[:].bitcast(FP8X4), scales=scales[:], in_=woven[1, q].bitcast(BF16))
            page_codes[1, q] = (codes[:], scales[:])

        call_codes.append(shelf.tile([P, S2], U32, name="call_codes0", align_bytes=64, offset=WGS_AT))
        lower_scales = shelf.tile([P, T2], U8, name="lower_scales", align_bytes=64, offset=WGS_AT + 4 * S2)
        gather_call_words(0, 0)
        for i in range(CHUNKS // 2):
            quantise_lower(i)
        gather_call_words(0, 1)
        for place, q in enumerate(ORDER):
            turn_back(1, q, (4 + 2 * place) % 8, nc.vector.tensor_copy if q == VECTOR_CHUNK else nc.scalar.copy)
        for q in ORDER:
            quantise_upper(q)
        call_codes.append(late.tile([P, S2], U32, name="call_codes1", align_bytes=64, offset=LAST_CALLS))
        for a in range(PASSES):
            gather_call_words(1, a)

        def score_bank(n, q):
            return banks[(CHUNKS * (n + 1) + ORDER.index(q)) % 8]

        def product(n, q, a):
            codes, scales = page_codes[a, q]
            half, c0 = n // 2, P * (n % 2)
            nc.tensor.matmul_mx(
                out=score_bank(n, q)[:],
                lhsT=call_codes[half][:, HALF_CALLS * a + c0 : HALF_CALLS * a + c0 + P].bitcast(FP8X4),
                lhsT_scale=call_scales[4 * a : P, P * n : P * (n + 1)],
                rhs=codes.bitcast(FP8X4), rhs_scale=scales, start=(a == 0), stop=(a == PASSES - 1),
            )

        def scores(n):
            e = ring.tile([P, T2], F32, name="e", tag="rows", bufs=PAGES)
            for q in ORDER:
                for a in range(PASSES):
                    product(n, q, a)
                nc.scalar.copy(out=e[:, BANK * q : BANK * (q + 1)], in_=score_bank(n, q)[:])
            return e


        def finish(piece, n, first, width, e):
            picked = keep.tile([P, width], F32, name="picked%d" % piece)
            nc.vector.tensor_copy(picked[:], e[:].indirect(part_of(read_list, first, width)))
            bound = floor[:, n : n + 1]
            if piece < SQUARE_ON_GPSIMD:
                result = keep.tile([P, width], F32, name="result%d" % piece)
                nc.gpsimd.tensor_scalar(picked[:], picked[:], FLOAT_MAX, bound, ALU.min, ALU.max)
                nc.gpsimd.tensor_tensor(result[:], picked[:], picked[:], ALU.mult)
            elif piece < len(pieces) - 1:
                at = LAST_CALLS + 64 + 4 * BANK * (piece - SQUARE_ON_GPSIMD - 1)
                result = late.tile([P, width], F32, name="result%d" % piece, align_bytes=64, offset=at)
                nc.gpsimd.tensor_scalar(picked[:], picked[:], FLOAT_MAX, bound, ALU.min, ALU.max)
                nc.scalar.activation(out=result[:], in_=picked[:], func=ACT.Square)
            else:
                result = keep.tile([P, width], F32, name="result%d" % piece)
                nc.vector.tensor_scalar(picked[:], picked[:], bound, None, ALU.max)
                nc.vector.tensor_tensor(result[:], picked[:], picked[:], ALU.mult)
            nc.sync.dma_start(out=out[P * n : P * (n + 1), first : first + width], in_=result[:])

        score_tiles = [scores(n) for n in range(CALL_TILES)]
        pieces = [(n, first, BANK) for n in range(CALL_TILES) for first in range(0, PICKS, BANK)]
        pieces = pieces[:-1] + [(CALL_TILES - 1, BANK, BANK - LAST_PIECE), (CALL_TILES - 1, PICKS - LAST_PIECE, LAST_PIECE)]
        for piece, (n, first, width) in enumerate(pieces):
            finish(piece, n, first, width, score_tiles[n])
